import numpy as np
import ml_dtypes


def mxq(x, axis, fmt="e4m3"):
    dtype, down = {"e4m3": (ml_dtypes.float8_e4m3fn, 7), "e5m2": (ml_dtypes.float8_e5m2, 14)}[fmt]
    v = np.moveaxis(np.asarray(x, np.float32).astype(ml_dtypes.bfloat16).astype(np.float64), axis, -1)
    blocks = v.reshape(v.shape[:-1] + (-1, 32))
    amax = np.abs(blocks).max(-1, keepdims=True)
    byte = np.maximum(np.where(amax > 0, np.frexp(amax)[1] - 1 + 127, 0) - down, 1)
    scale = np.exp2(byte - 127.0)
    codes = (blocks / scale).astype(np.float32).astype(dtype).astype(np.float64)
    return np.moveaxis((codes * scale).reshape(v.shape), -1, axis)


WIDE = False


def mx_kscale(k):
    if not WIDE:
        return np.ones(k)
    levels = np.array([10, -10, 5, -5, 0])
    if k % 512:
        return np.exp2(np.random.permutation(np.resize(levels, k // 32))).repeat(32)
    a = np.empty((k // 512, 16))
    for p in range(k // 512):
        a[p, :8] = np.random.permutation(np.resize(levels, 8))
        for g in range(8):
            far = levels[np.abs(levels - a[p, g]) >= 10]
            a[p, g + 8] = far[np.random.randint(len(far))]
    return np.exp2(a.ravel()).repeat(32)


def f64(x):
    return np.asarray(x).astype(np.float64)


def striped(idx):
    return np.tile(idx.reshape(-1, 16).T, (8, 1)).astype(np.uint16)


def unstriped(offs):
    return offs[:16].T.reshape(-1).astype(np.int64)


E2M1 = np.array([0.0, 0.5, 1.0, 1.5, 2.0, 3.0, 4.0, 6.0, -0.0, -0.5, -1.0, -1.5, -2.0, -3.0, -4.0, -6.0])


def pack_weight(w, fmt):
    k, n = w.shape
    w = f64(np.asarray(w, np.float32).astype(ml_dtypes.bfloat16)).reshape(k // 32, 32, n)
    amax = np.abs(w).max(1)
    if fmt == "e4m3":
        byte = np.frexp(amax)[1] - 1 + 127 - 7
    else:
        mant, ex = np.frexp(amax / 6.0)
        byte = np.where(mant > 0.5, ex, ex - 1) + 127
    byte = np.clip(np.where(amax > 0, byte, 1), 1, 254)
    scaled = (w * np.exp2(127.0 - byte)[:, None, :]).reshape(k, n).astype(np.float32)
    by_word = np.ascontiguousarray(scaled.reshape(k // 512, 128, 4, n).transpose(0, 1, 3, 2))
    if fmt == "e4m3":
        words = by_word.astype(ml_dtypes.float8_e4m3fn).view(np.uint8)
    else:
        c = by_word.astype(ml_dtypes.float4_e2m1fn).view(np.uint8) & 0xF
        words = (c[..., 0::2] | (c[..., 1::2] << 4)).reshape(k // 512, 128, 2 * n)
    return np.ascontiguousarray(words), np.ascontiguousarray(byte.astype(np.uint8).reshape(k // 512, 16, n))


def unpack_weight(words, scales, fmt):
    g, _, n = scales.shape
    words = np.ascontiguousarray(words).reshape(g, 128, n, -1)
    if fmt == "e4m3":
        vals = words.view(ml_dtypes.float8_e4m3fn).astype(np.float64)
    else:
        nib = np.empty((g, 128, n, 4), np.uint8)
        nib[..., 0::2] = words & 0xF
        nib[..., 1::2] = words >> 4
        vals = E2M1[nib]
    vals = vals * np.repeat(np.exp2(scales.astype(np.float64) - 127.0), 8, axis=1)[..., None]
    return vals.transpose(0, 1, 3, 2).reshape(g * 512, n)


def gelu(v):
    return 0.5 * v * (1.0 + np.tanh(np.sqrt(2.0 / np.pi) * (v + 0.044715 * v**3)))


def bf(x):
    return np.asarray(x, np.float32).astype(ml_dtypes.bfloat16)


def planes(Y):
    n, m = Y.shape
    b = f64(bf(Y)).reshape(n // 32, 32, m)
    amax = np.abs(b).max(1)
    byte = np.clip(np.where(amax > 0, np.frexp(amax)[1] - 1 + 127 - 7, 1), 1, 254)
    codes = (b * np.exp2(127.0 - byte)[:, None, :]).reshape(n, m).astype(np.float32).astype(ml_dtypes.float8_e4m3fn).view(np.uint8)
    words = codes.reshape(n // 512, 128, 4, m).transpose(0, 1, 3, 2)
    return np.ascontiguousarray(words), np.ascontiguousarray(byte.astype(np.uint8).reshape(n // 512, 16, m))


K, T, S, H, N = 512, 4096, 1024, 1024, 512

def setup_inputs():
    n = np.random.standard_normal
    s = mx_kscale(K)[:, None]
    u = mx_kscale(H)[:, None]
    tab_words, tab_scales = pack_weight(n((K, T)) * s, "e4m3")
    offs = striped(np.random.permutation(T)[:S])
    w1 = (n((K, H)) / np.sqrt(K) / s).astype(np.float32)
    w2_words, w2_scales = pack_weight(0.8 * n((K, H)) / np.sqrt(K) / s * u.T, "e2m1")
    gain = (np.exp(0.3 * n(H)) * u[:, 0]).astype(np.float32)
    w3 = (n((H, N)) / np.sqrt(H) / u).astype(np.float32)
    w4_words, w4_scales = pack_weight(n((H, N)) / np.sqrt(H) / u, "e4m3")
    base = (0.7 * n((N, S))).astype(np.float32)
    return {"tab_words": tab_words, "tab_scales": tab_scales, "offs": offs,
            "w1": w1, "w2_words": w2_words, "w2_scales": w2_scales, "gain": gain,
            "w3": w3, "w4_words": w4_words, "w4_scales": w4_scales, "base": base}

def reference(tab_words, tab_scales, offs, w1, w2_words, w2_scales, gain,
              w3, w4_words, w4_scales, base):
    v = unpack_weight(tab_words, tab_scales, "e4m3")[:, unstriped(offs)]
    a = mxq(f64(w1), 0, "e4m3").T @ v
    b = unpack_weight(w2_words, w2_scales, "e2m1").T @ v
    h = f64(gain)[:, None] * (a / np.hypot(1.0, a)) + b
    words, scales = planes(h)
    hq = mxq(h, 0, "e4m3")
    d = mxq(f64(w3), 0, "e4m3").T @ hq
    e = unpack_weight(w4_words, w4_scales, "e4m3").T @ hq
    y = d * e - f64(base)
    return y, h, words, scales

@@ -1,0 +1,266 @@
+from contextlib import ExitStack
+
+import concourse.mybir as mybir
+
+K, T, S, H, N = 512, 4096, 1024, 1024, 512
+FLOPS = 2 * (2 * K * H * S + 2 * H * N * S)
+
+F32 = mybir.dt.float32
+BF16 = mybir.dt.bfloat16
+I32 = mybir.dt.int32
+U32 = mybir.dt.uint32
+U16 = mybir.dt.uint16
+U8 = mybir.dt.uint8
+FP8X4 = mybir.dt.float8_e4m3fn_x4
+FP4X4 = mybir.dt.float4_e2m1fn_x4
+ACT = mybir.ActivationFunctionType
+ALU = mybir.AluOpType
+
+P = 128
+PACK = 4
+PASS = P * PACK
+BANK = 512
+GROUPS = H // PASS
+HALF = 512
+CHUNKS = [(0, 512), (512, 256), (768, 128), (896, 128)]
+POOL_PIECE = 128
+H_ROUND = ["gg","gg","vv","vv"]
+SUB = "ggvv"
+W3_ROUND = "gg"
+
+
+def tile_list_book_impact_kernel(tc, tab_words, tab_scales, offs, w1, w2_words, w2_scales, gain,
+                                          w3, w4_words, w4_scales, base, out_0, out_1, out_2, out_3):
+    nc = tc.nc
+    with ExitStack() as ctx:
+        keep = ctx.enter_context(tc.tile_pool(name="keep", bufs=1))
+        ring = ctx.enter_context(tc.tile_pool(name="ring", bufs=3))
+        psum = ctx.enter_context(tc.psum_pool(name="psum", bufs=1))
+
+        offsets = keep.tile([P, S // 16], U16, name="offsets")
+        nc.sync.dma_start(offsets[:], offs)
+
+        w2_w = keep.tile([P, 2 * H], U8, name="w2_w", tag="slot_a", align_bytes=64)
+        nc.sync.dma_start(out=w2_w[:].bitcast(I32), in_=w2_words[0].bitcast(I32))
+        tab_w = keep.tile([P, T], I32, name="tab_w", tag="slot_t", align_bytes=64)
+        nc.sync.dma_start(out=tab_w[:], in_=tab_words[0].rearrange("p n t -> p (n t)").bitcast(I32))
+        tab_s = keep.tile([P, T], U8, name="tab_s", tag="slot_s", align_bytes=64)
+        nc.vector.memset(tab_s[:].bitcast(I32), 0)
+        for q in range(4):
+            nc.sync.dma_start(out=tab_s[32 * q : 32 * q + 4, :].bitcast(I32),
+                              in_=tab_scales[0, 4 * q : 4 * q + 4, :].bitcast(I32))
+
+        w2_s = keep.tile([P, H], U8, name="w2_s", tag="slot_b", align_bytes=64)
+        nc.gpsimd.memset(w2_s[:].bitcast(I32), 0)
+        for q in range(4):
+            nc.gpsimd.dma_start(out=w2_s[32 * q : 32 * q + 4, :].bitcast(I32),
+                                in_=w2_scales[0, 4 * q : 4 * q + 4, :].bitcast(I32))
+
+        one = keep.tile([P, 1], F32, name="one")
+        nc.vector.memset(one[:], 1.0)
+        warm = keep.tile([P, 1], F32, name="warm")
+        nc.scalar.activation(warm[:], one[:], ACT.Abs_reciprocal_sqrt)
+
+        gain_s = keep.tile([P, GROUPS, PACK], F32, name="gain_s")
+        nc.gpsimd.dma_start(out=gain_s[:], in_=gain.rearrange("(g p t) -> p g t", g=GROUPS, t=PACK))
+        w4_s = keep.tile([P, GROUPS, N], U8, name="w4_s", align_bytes=64)
+        for q in range(4):
+            nc.gpsimd.dma_start(out=w4_s[32 * q : 32 * q + 4, :, :].bitcast(I32),
+                                in_=w4_scales[:, 4 * q : 4 * q + 4, :].rearrange("g r n -> r g n").bitcast(I32))
+
+        w1_rows = w1.rearrange("(p j) c -> p j c", j=PACK)
+        base_rows = base.rearrange("(i p) s -> p i s", p=P)
+        w1_raw, w3_raw, base_sb, w4_w = {}, {}, {}, {}
+
+        def load_w1(g):
+            w1_raw[g] = keep.tile([P, 2, PACK, 256], F32, name="w1_raw%d" % g, tag=("slot_a", "slot_b")[g], align_bytes=64)
+            for u in range(2):
+                c = PASS * g + 256 * u
+                nc.sync.dma_start(out=w1_raw[g][:, u], in_=w1_rows[:, :, c : c + 256])
+
+        def load_w3(g):
+            w3_raw[g] = keep.tile([P, PACK, N], F32, name="w3_raw%d" % g, tag=("slot_t", "slot_a")[g], align_bytes=64)
+            nc.sync.dma_start(out=w3_raw[g][:],
+                              in_=w3[PASS * g : PASS * (g + 1), :].rearrange("(p j) n -> p j n", j=PACK))
+
+        def load_w4():
+            w4_w[0] = keep.tile([P, GROUPS, N], I32, name="w4_w", tag="slot_s", align_bytes=64)
+            nc.sync.dma_start(out=w4_w[0][:], in_=w4_words.rearrange("g p n t -> p g (n t)").bitcast(I32))
+
+        def load_base(half):
+            base_sb[half] = keep.tile([P, N // P, HALF], F32, name="base%d" % half, tag=("slot_b", "slot_t")[half],
+                                      align_bytes=64)
+            nc.sync.dma_start(out=base_sb[half][:], in_=base_rows[:, :, HALF * half : HALF * (half + 1)])
+
+        v_s = [keep.tile([P, HALF], U8, name="v_s%d" % half, align_bytes=64) for half in range(2)]
+        v_w = [keep.tile([P, HALF], U32, name="v_w%d" % half, align_bytes=64) for half in range(2)]
+
+        def gather_scales(half):
+            nc.vector.tensor_copy(v_s[half][:], tab_s[:].indirect(offsets[:, 32 * half : 32 * (half + 1)]))
+
+        def gather_words(half):
+            nc.vector.tensor_copy(v_w[half][:], tab_w[:].bitcast(U32).indirect(offsets[:, 32 * half : 32 * (half + 1)]))
+
+        w2_wp = [keep.tile([P, 2 * PASS], U8, name="w2_wp%d" % g, align_bytes=64) for g in range(GROUPS)]
+        w2_sp = [keep.tile([P, PASS], U8, name="w2_sp%d" % g, align_bytes=64) for g in range(GROUPS)]
+
+        def deal_w2_words(g):
+            nc.vector.tensor_copy(
+                w2_wp[g][:].bitcast(U16).rearrange("p (t m) -> p t m", t=PACK),
+                w2_w[:, 2 * PASS * g : 2 * PASS * (g + 1)].bitcast(U16).rearrange("p (m t) -> p t m", t=PACK))
+
+        def deal_w2_scales(g):
+            nc.vector.tensor_copy(
+                w2_sp[g][:].rearrange("p (t m) -> p t m", t=PACK),
+                w2_s[:, PASS * g : PASS * (g + 1)].rearrange("p (m t) -> p t m", t=PACK))
+
+        w1_q = [keep.tile([P, PASS], U32, name="w1_q%d" % g, align_bytes=64) for g in range(GROUPS)]
+        w1_s = [keep.tile([P, PASS], U8, name="w1_s%d" % g, align_bytes=64) for g in range(GROUPS)]
+        w1_b = [keep.tile([P, PACK * PASS], BF16, name="w1_b%d" % g, align_bytes=64) for g in range(GROUPS)]
+
+        def round_w1(g):
+            dealt = w1_b[g][:].rearrange("p (t m j) -> p m t j", t=PACK, j=PACK)
+            for u in range(2):
+                nc.scalar.copy(dealt[:, 64 * u : 64 * (u + 1)],
+                               w1_raw[g][:, u].rearrange("p j (m t) -> p m t j", t=PACK))
+
+        def quantise_w1(g):
+            nc.vector.quantize_mx(out=w1_q[g][:].bitcast(FP8X4), scales=w1_s[g][:], in_=w1_b[g][:])
+
+        w3_q = [keep.tile([P, N], U32, name="w3_q%d" % g, align_bytes=64) for g in range(GROUPS)]
+        w3_s = [keep.tile([P, N], U8, name="w3_s%d" % g, align_bytes=64) for g in range(GROUPS)]
+        w3_b = [keep.tile([P, N, PACK], BF16, name="w3_b%d" % g, align_bytes=64) for g in range(GROUPS)]
+
+        def pool_round(dst, src, width):
+            for c in range(0, width, POOL_PIECE):
+                nc.gpsimd.tensor_scalar(dst[:, c : c + POOL_PIECE, :],
+                                        src[:, :, c : c + POOL_PIECE].rearrange("p j n -> p n j"),
+                                        1.0, 0.0, ALU.mult, ALU.add)
+
+        def round_on(engine, dst, src, width):
+            if engine == "g":
+                pool_round(dst, src, width)
+            elif engine == "s":
+                for c in range(0, width, 128):
+                    nc.scalar.copy(dst[:, c : c + 128, :], src[:, :, c : c + 128].rearrange("p j n -> p n j"))
+            else:
+                nc.vector.tensor_copy(dst[:], src[:].rearrange("p t s -> p s t"))
+
+        def prepare_w3(g):
+            round_on(W3_ROUND[g], w3_b[g], w3_raw[g], N)
+            nc.vector.quantize_mx(out=w3_q[g][:].bitcast(FP8X4), scales=w3_s[g][:],
+                                  in_=w3_b[g][:].rearrange("p n j -> p (n j)"))
+
+        h_s = keep.tile([P, GROUPS * S], U8, name="h_s", align_bytes=64)
+
+        def first_stage(n, c0, width, g, h_q):
+            half, v0 = divmod(c0, HALF)
+            v_words = v_w[half][:, v0 : v0 + width].bitcast(FP8X4)
+            v_scales = v_s[half][:, v0 : v0 + width]
+            per_bank = BANK // width
+            h = keep.tile([P, PACK, width], F32, name="h_%d_%d" % (c0, g))
+            for t0 in range(0, PACK, per_bank):
+                a = psum.tile([P, per_bank, width], F32, name="a", bufs=3)
+                b = psum.tile([P, per_bank, width], F32, name="b", bufs=2)
+                for i in range(per_bank):
+                    t = t0 + i
+                    nc.tensor.matmul_mx(out=a[:, i, :], lhsT=w1_q[g][:, P * t : P * (t + 1)].bitcast(FP8X4),
+                                        lhsT_scale=w1_s[g][:, P * t : P * (t + 1)],
+                                        rhs=v_words, rhs_scale=v_scales, start=True, stop=True)
+                for i in range(per_bank):
+                    t = t0 + i
+                    nc.tensor.matmul_mx(out=b[:, i, :], lhsT=w2_wp[g][:, 2 * P * t : 2 * P * (t + 1)].bitcast(FP4X4),
+                                        lhsT_scale=w2_sp[g][:, P * t : P * (t + 1)],
+                                        rhs=v_words, rhs_scale=v_scales, start=True, stop=True)
+                square = ring.tile([P, per_bank, width], F32, name="square")
+                nc.scalar.activation(square[:], a[:], ACT.Square)
+                root = ring.tile([P, per_bank, width], F32, name="root")
+                nc.scalar.activation(root[:], square[:], ACT.Abs_reciprocal_sqrt, bias=one[:])
+                sat = ring.tile([P, per_bank, width], F32, name="sat")
+                for i in range(per_bank):
+                    t = t0 + i
+                    nc.vector.scalar_tensor_tensor(sat[:, i, :], a[:, i, :], gain_s[:, g, t : t + 1], root[:, i, :],
+                                                   ALU.mult, ALU.mult)
+                nc.vector.tensor_tensor(h[:, t0 : t0 + per_bank, :], sat[:], b[:], ALU.add)
+            nc.sync.dma_start(
+                out=out_1[PASS * g : PASS * (g + 1), c0 : c0 + width].rearrange("(p t) s -> p t s", t=PACK), in_=h[:])
+            h_b = ring.tile([P, width, PACK], BF16, name="h_b", align_bytes=64)
+            round_on(H_ROUND[n][g], h_b, h, width)
+            nc.vector.quantize_mx(out=h_q[:, g, :].bitcast(FP8X4), scales=h_s[:, S * g + c0 : S * g + c0 + width],
+                                  in_=h_b[:].rearrange("p s t -> p (s t)"))
+
+        def second_stage(n, c0, width, h_q):
+            half, v0 = divmod(c0, HALF)
+            per_bank = BANK // width
+            nc.sync.dma_start(
+                out=out_2[:, :, c0 : c0 + width, :].rearrange("g p m t -> p g (m t)").bitcast(I32),
+                in_=h_q[:].bitcast(I32))
+            y = keep.tile([P, N // P, width], F32, name="y_%d" % c0)
+            y_rows = out_0.rearrange("(i p) s -> p i s", p=P)
+            for i0 in range(0, N // P, per_bank):
+                d = psum.tile([P, per_bank, width], F32, name="d", bufs=1)
+                e = psum.tile([P, per_bank, width], F32, name="e", bufs=2)
+                for i in range(per_bank):
+                    cols = slice(P * (i0 + i), P * (i0 + i + 1))
+                    for g in range(GROUPS):
+                        nc.tensor.matmul_mx(out=d[:, i, :], lhsT=w3_q[g][:, cols].bitcast(FP8X4), lhsT_scale=w3_s[g][:, cols],
+                                            rhs=h_q[:, g, :].bitcast(FP8X4),
+                                            rhs_scale=h_s[:, S * g + c0 : S * g + c0 + width],
+                                            start=(g == 0), stop=(g == GROUPS - 1))
+                for i in range(per_bank):
+                    cols = slice(P * (i0 + i), P * (i0 + i + 1))
+                    for g in range(GROUPS):
+                        nc.tensor.matmul_mx(out=e[:, i, :], lhsT=w4_w[0][:, g, cols].bitcast(FP8X4), lhsT_scale=w4_s[:, g, cols],
+                                            rhs=h_q[:, g, :].bitcast(FP8X4),
+                                            rhs_scale=h_s[:, S * g + c0 : S * g + c0 + width],
+                                            start=(g == 0), stop=(g == GROUPS - 1))
+                d_sb = ring.tile([P, per_bank, width], F32, name="d_sb")
+                nc.scalar.copy(d_sb[:], d[:])
+                prod = ring.tile([P, per_bank, width], F32, name="prod")
+                nc.vector.tensor_tensor(prod[:], d_sb[:], e[:], ALU.mult)
+                rows = slice(i0, i0 + per_bank)
+                base_part = base_sb[half][:, rows, v0 : v0 + width]
+                if SUB[n] == "g":
+                    for u in range(2):
+                        w2 = width // 2
+                        nc.gpsimd.tensor_tensor(y[:, rows, w2 * u : w2 * (u + 1)], prod[:, :, w2 * u : w2 * (u + 1)],
+                                                base_part[:, :, w2 * u : w2 * (u + 1)], ALU.subtract)
+                else:
+                    nc.vector.tensor_tensor(y[:, rows, :], prod[:], base_part, ALU.subtract)
+                done = i0 + per_bank
+                if done % 2 == 0:
+                    first = max(0, done - max(2, per_bank))
+                    nc.sync.dma_start(out=y_rows[:, first:done, c0 : c0 + width], in_=y[:, first:done, :])
+
+        deal_w2_words(0)
+        deal_w2_words(1)
+        load_w1(0)
+        deal_w2_scales(0)
+        deal_w2_scales(1)
+        load_w1(1)
+        gather_words(0)
+        gather_scales(0)
+        round_w1(0)
+        quantise_w1(0)
+        gather_words(1)
+        load_w3(0)
+        load_w3(1)
+        gather_scales(1)
+        load_w4()
+        for n, (c0, width) in enumerate(CHUNKS):
+            h_q = keep.tile([P, GROUPS, width], U32, name="h_q%d" % c0, align_bytes=64)
+            for g in range(GROUPS):
+                if n == 0 and g == 1:
+                    round_w1(1)
+                    quantise_w1(1)
+                    load_base(0)
+                first_stage(n, c0, width, g, h_q)
+                if n == 0:
+                    prepare_w3(g)
+                if n == 0 and g == 0:
+                    load_base(1)
+            second_stage(n, c0, width, h_q)
+        for q in range(4):
+            nc.sync.dma_start(
+                out=out_3[:, 4 * q : 4 * q + 4, :].rearrange("g r m -> r g m").bitcast(I32),
+                in_=h_s[32 * q : 32 * q + 4, :].bitcast(I32).rearrange("r (g m) -> r g m", g=GROUPS))

@@ -24,9 +24,10 @@ GROUPS = H // PASS
 HALF = 512
 CHUNKS = [(0, 512), (512, 256), (768, 128), (896, 128)]
 POOL_PIECE = 128
-H_ROUND = ["gg","gg","vv","vv"]
-SUB = "ggvv"
-W3_ROUND = "gg"
+H_ROUND = ["vs","ss","ss","vv"]
+SUB = "vvvv"
+W3_ROUND = "vs"
+W1_ROUND = ["sv","ss"]
 
 
 def tile_list_book_impact_kernel(tc, tab_words, tab_scales, offs, w1, w2_words, w2_scales, gain,
@@ -40,24 +41,27 @@ def tile_list_book_impact_kernel(tc, tab_words, tab_scales, offs, w1, w2_words, 
         offsets = keep.tile([P, S // 16], U16, name="offsets")
         nc.sync.dma_start(offsets[:], offs)
 
-        w2_w = keep.tile([P, 2 * H], U8, name="w2_w", tag="slot_a", align_bytes=64)
-        nc.sync.dma_start(out=w2_w[:].bitcast(I32), in_=w2_words[0].bitcast(I32))
+        w2_w = []
+        for g in range(GROUPS):
+            words = keep.tile([P, 2 * PASS], U8, name="w2_w%d" % g, tag=("slot_a", "slot_b")[g], align_bytes=64)
+            nc.sync.dma_start(out=words[:].bitcast(I32), in_=w2_words[0, :, 2 * PASS * g : 2 * PASS * (g + 1)].bitcast(I32))
+            w2_w.append(words)
         tab_w = keep.tile([P, T], I32, name="tab_w", tag="slot_t", align_bytes=64)
         nc.sync.dma_start(out=tab_w[:], in_=tab_words[0].rearrange("p n t -> p (n t)").bitcast(I32))
         tab_s = keep.tile([P, T], U8, name="tab_s", tag="slot_s", align_bytes=64)
         nc.vector.memset(tab_s[:].bitcast(I32), 0)
         for q in range(4):
-            nc.sync.dma_start(out=tab_s[32 * q : 32 * q + 4, :].bitcast(I32),
-                              in_=tab_scales[0, 4 * q : 4 * q + 4, :].bitcast(I32))
+            nc.scalar.dma_start(out=tab_s[32 * q : 32 * q + 4, :].bitcast(I32),
+                                in_=tab_scales[0, 4 * q : 4 * q + 4, :].bitcast(I32))
 
-        w2_s = keep.tile([P, H], U8, name="w2_s", tag="slot_b", align_bytes=64)
-        nc.gpsimd.memset(w2_s[:].bitcast(I32), 0)
+        w2_s = keep.tile([P, H], U8, name="w2_s", align_bytes=64)
+        nc.vector.memset(w2_s[:].bitcast(I32), 0)
         for q in range(4):
-            nc.gpsimd.dma_start(out=w2_s[32 * q : 32 * q + 4, :].bitcast(I32),
+            nc.scalar.dma_start(out=w2_s[32 * q : 32 * q + 4, :].bitcast(I32),
                                 in_=w2_scales[0, 4 * q : 4 * q + 4, :].bitcast(I32))
 
         one = keep.tile([P, 1], F32, name="one")
-        nc.vector.memset(one[:], 1.0)
+        nc.gpsimd.memset(one[:], 1.0)
         warm = keep.tile([P, 1], F32, name="warm")
         nc.scalar.activation(warm[:], one[:], ACT.Abs_reciprocal_sqrt)
 
@@ -107,7 +111,7 @@ def tile_list_book_impact_kernel(tc, tab_words, tab_scales, offs, w1, w2_words, 
         def deal_w2_words(g):
             nc.vector.tensor_copy(
                 w2_wp[g][:].bitcast(U16).rearrange("p (t m) -> p t m", t=PACK),
-                w2_w[:, 2 * PASS * g : 2 * PASS * (g + 1)].bitcast(U16).rearrange("p (m t) -> p t m", t=PACK))
+                w2_w[g][:].bitcast(U16).rearrange("p (m t) -> p t m", t=PACK))
 
         def deal_w2_scales(g):
             nc.vector.tensor_copy(
@@ -121,8 +125,12 @@ def tile_list_book_impact_kernel(tc, tab_words, tab_scales, offs, w1, w2_words, 
         def round_w1(g):
             dealt = w1_b[g][:].rearrange("p (t m j) -> p m t j", t=PACK, j=PACK)
             for u in range(2):
-                nc.scalar.copy(dealt[:, 64 * u : 64 * (u + 1)],
-                               w1_raw[g][:, u].rearrange("p j (m t) -> p m t j", t=PACK))
+                raw = w1_raw[g][:, u].rearrange("p j (m t) -> p m t j", t=PACK)
+                if W1_ROUND[g][u] == "v":
+                    nc.vector.tensor_copy(dealt[:, 64 * u : 64 * (u + 1)], raw)
+                else:
+                    for m in range(0, 64, 32):
+                        nc.scalar.copy(dealt[:, 64 * u + m : 64 * u + m + 32], raw[:, m : m + 32])
 
         def quantise_w1(g):
             nc.vector.quantize_mx(out=w1_q[g][:].bitcast(FP8X4), scales=w1_s[g][:], in_=w1_b[g][:])
@@ -146,120 +154,148 @@ def tile_list_book_impact_kernel(tc, tab_words, tab_scales, offs, w1, w2_words, 
             else:
                 nc.vector.tensor_copy(dst[:], src[:].rearrange("p t s -> p s t"))
 
-        def prepare_w3(g):
+        def round_w3(g):
             round_on(W3_ROUND[g], w3_b[g], w3_raw[g], N)
+
+        def quantise_w3(g):
             nc.vector.quantize_mx(out=w3_q[g][:].bitcast(FP8X4), scales=w3_s[g][:],
                                   in_=w3_b[g][:].rearrange("p n j -> p (n j)"))
 
         h_s = keep.tile([P, GROUPS * S], U8, name="h_s", align_bytes=64)
 
-        def first_stage(n, c0, width, g, h_q):
+        y_rows = out_0.rearrange("(i p) s -> p i s", p=P)
+        later = {}
+
+        def at(step, work, *args):
+            later.setdefault(step, []).append((work, args))
+
+        def moving_v(c0, width):
             half, v0 = divmod(c0, HALF)
-            v_words = v_w[half][:, v0 : v0 + width].bitcast(FP8X4)
-            v_scales = v_s[half][:, v0 : v0 + width]
+            return v_w[half][:, v0 : v0 + width].bitcast(FP8X4), v_s[half][:, v0 : v0 + width]
+
+        def saturate(c0, width, g, t0):
+            v_words, v_scales = moving_v(c0, width)
             per_bank = BANK // width
-            h = keep.tile([P, PACK, width], F32, name="h_%d_%d" % (c0, g))
-            for t0 in range(0, PACK, per_bank):
-                a = psum.tile([P, per_bank, width], F32, name="a", bufs=3)
-                b = psum.tile([P, per_bank, width], F32, name="b", bufs=2)
-                for i in range(per_bank):
-                    t = t0 + i
-                    nc.tensor.matmul_mx(out=a[:, i, :], lhsT=w1_q[g][:, P * t : P * (t + 1)].bitcast(FP8X4),
-                                        lhsT_scale=w1_s[g][:, P * t : P * (t + 1)],
-                                        rhs=v_words, rhs_scale=v_scales, start=True, stop=True)
-                for i in range(per_bank):
-                    t = t0 + i
-                    nc.tensor.matmul_mx(out=b[:, i, :], lhsT=w2_wp[g][:, 2 * P * t : 2 * P * (t + 1)].bitcast(FP4X4),
-                                        lhsT_scale=w2_sp[g][:, P * t : P * (t + 1)],
-                                        rhs=v_words, rhs_scale=v_scales, start=True, stop=True)
-                square = ring.tile([P, per_bank, width], F32, name="square")
-                nc.scalar.activation(square[:], a[:], ACT.Square)
-                root = ring.tile([P, per_bank, width], F32, name="root")
-                nc.scalar.activation(root[:], square[:], ACT.Abs_reciprocal_sqrt, bias=one[:])
-                sat = ring.tile([P, per_bank, width], F32, name="sat")
-                for i in range(per_bank):
-                    t = t0 + i
-                    nc.vector.scalar_tensor_tensor(sat[:, i, :], a[:, i, :], gain_s[:, g, t : t + 1], root[:, i, :],
-                                                   ALU.mult, ALU.mult)
-                nc.vector.tensor_tensor(h[:, t0 : t0 + per_bank, :], sat[:], b[:], ALU.add)
-            nc.sync.dma_start(
-                out=out_1[PASS * g : PASS * (g + 1), c0 : c0 + width].rearrange("(p t) s -> p t s", t=PACK), in_=h[:])
-            h_b = ring.tile([P, width, PACK], BF16, name="h_b", align_bytes=64)
-            round_on(H_ROUND[n][g], h_b, h, width)
+            a = psum.tile([P, per_bank, width], F32, name="a", bufs=3)
+            for i in range(per_bank):
+                t = t0 + i
+                nc.tensor.matmul_mx(out=a[:, i, :], lhsT=w1_q[g][:, P * t : P * (t + 1)].bitcast(FP8X4),
+                                    lhsT_scale=w1_s[g][:, P * t : P * (t + 1)],
+                                    rhs=v_words, rhs_scale=v_scales, start=True, stop=True)
+            square = ring.tile([P, per_bank, width], F32, name="square")
+            nc.scalar.activation(square[:], a[:], ACT.Square)
+            root = ring.tile([P, per_bank, width], F32, name="root")
+            nc.scalar.activation(root[:], square[:], ACT.Abs_reciprocal_sqrt, bias=one[:])
+            sat = ring.tile([P, per_bank, width], F32, name="sat")
+            for i in range(per_bank):
+                t = t0 + i
+                nc.vector.scalar_tensor_tensor(sat[:, i, :], a[:, i, :], gain_s[:, g, t : t + 1], root[:, i, :],
+                                               ALU.mult, ALU.mult)
+            return sat
+
+        def add_linear(c0, width, g, t0, sat, h):
+            v_words, v_scales = moving_v(c0, width)
+            per_bank = BANK // width
+            b = psum.tile([P, per_bank, width], F32, name="b", bufs=2)
+            for i in range(per_bank):
+                t = t0 + i
+                nc.tensor.matmul_mx(out=b[:, i, :], lhsT=w2_wp[g][:, 2 * P * t : 2 * P * (t + 1)].bitcast(FP4X4),
+                                    lhsT_scale=w2_sp[g][:, P * t : P * (t + 1)],
+                                    rhs=v_words, rhs_scale=v_scales, start=True, stop=True)
+            nc.vector.tensor_tensor(h[:, t0 : t0 + per_bank, :], sat[:], b[:], ALU.add)
+            if t0 + per_bank == PACK:
+                nc.sync.dma_start(
+                    out=out_1[PASS * g : PASS * (g + 1), c0 : c0 + width].rearrange("(p t) s -> p t s", t=PACK),
+                    in_=h[:])
+
+        def quantise_h(c0, width, g, h_b, h_q):
             nc.vector.quantize_mx(out=h_q[:, g, :].bitcast(FP8X4), scales=h_s[:, S * g + c0 : S * g + c0 + width],
                                   in_=h_b[:].rearrange("p s t -> p (s t)"))
+            if g == GROUPS - 1:
+                nc.sync.dma_start(
+                    out=out_2[:, :, c0 : c0 + width, :].rearrange("g p m t -> p g (m t)").bitcast(I32),
+                    in_=h_q[:].bitcast(I32))
 
-        def second_stage(n, c0, width, h_q):
+        def round_h(step, n, c0, width, g, h, h_q):
+            h_b = ring.tile([P, width, PACK], BF16, name="h_b", align_bytes=64)
+            round_on(H_ROUND[n][g], h_b, h, width)
+            at(step + 1, quantise_h, c0, width, g, h_b, h_q)
+
+        def readings(step, n, c0, width, i0, h_q, y):
+            per_bank = BANK // width
+            d = psum.tile([P, per_bank, width], F32, name="d", bufs=1)
+            e = psum.tile([P, per_bank, width], F32, name="e", bufs=2)
+            for bank, words, scales in ((d, [w3_q[g][:] for g in range(GROUPS)], [w3_s[g][:] for g in range(GROUPS)]),
+                                        (e, [w4_w[0][:, g, :] for g in range(GROUPS)], [w4_s[:, g, :] for g in range(GROUPS)])):
+                for i in range(per_bank):
+                    cols = slice(P * (i0 + i), P * (i0 + i + 1))
+                    for g in range(GROUPS):
+                        nc.tensor.matmul_mx(out=bank[:, i, :], lhsT=words[g][:, cols].bitcast(FP8X4),
+                                            lhsT_scale=scales[g][:, cols], rhs=h_q[:, g, :].bitcast(FP8X4),
+                                            rhs_scale=h_s[:, S * g + c0 : S * g + c0 + width],
+                                            start=(g == 0), stop=(g == GROUPS - 1))
+            d_sb = ring.tile([P, per_bank, width], F32, name="d_sb")
+            nc.scalar.copy(d_sb[:], d[:])
+            prod = ring.tile([P, per_bank, width], F32, name="prod")
+            nc.vector.tensor_tensor(prod[:], d_sb[:], e[:], ALU.mult)
+            at(step + 1, less_base, n, c0, width, i0, prod, y)
+
+        def less_base(n, c0, width, i0, prod, y):
             half, v0 = divmod(c0, HALF)
             per_bank = BANK // width
-            nc.sync.dma_start(
-                out=out_2[:, :, c0 : c0 + width, :].rearrange("g p m t -> p g (m t)").bitcast(I32),
-                in_=h_q[:].bitcast(I32))
-            y = keep.tile([P, N // P, width], F32, name="y_%d" % c0)
-            y_rows = out_0.rearrange("(i p) s -> p i s", p=P)
-            for i0 in range(0, N // P, per_bank):
-                d = psum.tile([P, per_bank, width], F32, name="d", bufs=1)
-                e = psum.tile([P, per_bank, width], F32, name="e", bufs=2)
-                for i in range(per_bank):
-                    cols = slice(P * (i0 + i), P * (i0 + i + 1))
-                    for g in range(GROUPS):
-                        nc.tensor.matmul_mx(out=d[:, i, :], lhsT=w3_q[g][:, cols].bitcast(FP8X4), lhsT_scale=w3_s[g][:, cols],
-                                            rhs=h_q[:, g, :].bitcast(FP8X4),
-                                            rhs_scale=h_s[:, S * g + c0 : S * g + c0 + width],
-                                            start=(g == 0), stop=(g == GROUPS - 1))
-                for i in range(per_bank):
-                    cols = slice(P * (i0 + i), P * (i0 + i + 1))
-                    for g in range(GROUPS):
-                        nc.tensor.matmul_mx(out=e[:, i, :], lhsT=w4_w[0][:, g, cols].bitcast(FP8X4), lhsT_scale=w4_s[:, g, cols],
-                                            rhs=h_q[:, g, :].bitcast(FP8X4),
-                                            rhs_scale=h_s[:, S * g + c0 : S * g + c0 + width],
-                                            start=(g == 0), stop=(g == GROUPS - 1))
-                d_sb = ring.tile([P, per_bank, width], F32, name="d_sb")
-                nc.scalar.copy(d_sb[:], d[:])
-                prod = ring.tile([P, per_bank, width], F32, name="prod")
-                nc.vector.tensor_tensor(prod[:], d_sb[:], e[:], ALU.mult)
-                rows = slice(i0, i0 + per_bank)
-                base_part = base_sb[half][:, rows, v0 : v0 + width]
-                if SUB[n] == "g":
-                    for u in range(2):
-                        w2 = width // 2
-                        nc.gpsimd.tensor_tensor(y[:, rows, w2 * u : w2 * (u + 1)], prod[:, :, w2 * u : w2 * (u + 1)],
-                                                base_part[:, :, w2 * u : w2 * (u + 1)], ALU.subtract)
-                else:
-                    nc.vector.tensor_tensor(y[:, rows, :], prod[:], base_part, ALU.subtract)
-                done = i0 + per_bank
-                if done % 2 == 0:
-                    first = max(0, done - max(2, per_bank))
-                    nc.sync.dma_start(out=y_rows[:, first:done, c0 : c0 + width], in_=y[:, first:done, :])
+            rows = slice(i0, i0 + per_bank)
+            engine = nc.gpsimd if SUB[n] == "g" else nc.vector
+            engine.tensor_tensor(y[:, rows, :], prod[:], base_sb[half][:, rows, v0 : v0 + width], ALU.subtract)
+            done = i0 + per_bank
+            if done % 2 == 0:
+                first = max(0, done - max(2, per_bank))
+                nc.sync.dma_start(out=y_rows[:, first:done, c0 : c0 + width], in_=y[:, first:done, :])
 
         deal_w2_words(0)
         deal_w2_words(1)
         load_w1(0)
-        deal_w2_scales(0)
-        deal_w2_scales(1)
         load_w1(1)
-        gather_words(0)
         gather_scales(0)
-        round_w1(0)
-        quantise_w1(0)
-        gather_words(1)
-        load_w3(0)
-        load_w3(1)
         gather_scales(1)
         load_w4()
+        gather_words(0)
+        round_w1(0)
+        quantise_w1(0)
+        deal_w2_scales(0)
+        gather_words(1)
+        deal_w2_scales(1)
+        load_w3(0)
+        load_w3(1)
+        at(1, round_w1, 1)
+        at(2, quantise_w1, 1)
+        at(2, load_base, 0)
+        at(3, round_w3, 0)
+        at(4, quantise_w3, 0)
+        at(4, load_base, 1)
+        at(5, round_w3, 1)
+        at(7, quantise_w3, 1)
+        step = 0
+
+        def tick(step):
+            for work, args in later.pop(step, []):
+                work(*args)
+
         for n, (c0, width) in enumerate(CHUNKS):
+            per_bank = BANK // width
             h_q = keep.tile([P, GROUPS, width], U32, name="h_q%d" % c0, align_bytes=64)
+            y = keep.tile([P, N // P, width], F32, name="y_%d" % c0)
             for g in range(GROUPS):
-                if n == 0 and g == 1:
-                    round_w1(1)
-                    quantise_w1(1)
-                    load_base(0)
-                first_stage(n, c0, width, g, h_q)
-                if n == 0:
-                    prepare_w3(g)
-                if n == 0 and g == 0:
-                    load_base(1)
-            second_stage(n, c0, width, h_q)
+                h = keep.tile([P, PACK, width], F32, name="h_%d_%d" % (c0, g))
+                for t0 in range(0, PACK, per_bank):
+                    sat = saturate(c0, width, g, t0)
+                    at(step + 1, add_linear, c0, width, g, t0, sat, h)
+                    tick(step)
+                    step = step + 1
+                at(step + 1, round_h, step + 1, n, c0, width, g, h, h_q)
+            for m, i0 in enumerate(range(0, N // P, per_bank)):
+                at(step + 3 + m, readings, step + 3 + m, n, c0, width, i0, h_q, y)
+        for tail in range(step, step + 8):
+            tick(tail)
         for q in range(4):
             nc.sync.dma_start(
                 out=out_3[:, 4 * q : 4 * q + 4, :].rearrange("g r m -> r g m").bitcast(I32),

@@ -22,12 +22,12 @@ PASS = P * PACK
 BANK = 512
 GROUPS = H // PASS
 HALF = 512
-CHUNKS = [(0, 512), (512, 256), (768, 128), (896, 128)]
+BLOCKS = [(0, 512, 0), (0, 256, 1), (256, 256, 1), (512, 256, 0), (512, 256, 1), (768, 128, 0), (768, 128, 1), (896, 128, 0), (896, 128, 1)]
 POOL_PIECE = 128
-H_ROUND = ["vs","ss","ss","vv"]
-SUB = "vvvv"
-W3_ROUND = "vs"
-W1_ROUND = ["sv","ss"]
+H_ROUND = "sssssssvv"
+SUB = "vvvvvvvvv"
+W3_ROUND = "vv"
+SCALE_STORES = {768: 0, 1024: 768}
 
 
 def tile_list_book_impact_kernel(tc, tab_words, tab_scales, offs, w1, w2_words, w2_scales, gain,
@@ -77,24 +77,22 @@ def tile_list_book_impact_kernel(tc, tab_words, tab_scales, offs, w1, w2_words, 
         w1_raw, w3_raw, base_sb, w4_w = {}, {}, {}, {}
 
         def load_w1(g):
-            w1_raw[g] = keep.tile([P, 2, PACK, 256], F32, name="w1_raw%d" % g, tag=("slot_a", "slot_b")[g], align_bytes=64)
-            for u in range(2):
-                c = PASS * g + 256 * u
-                nc.sync.dma_start(out=w1_raw[g][:, u], in_=w1_rows[:, :, c : c + 256])
+            w1_raw[g] = keep.tile([P, PACK, PASS], F32, name="w1_raw%d" % g, tag=("slot_a", "slot_b")[g], align_bytes=64)
+            nc.sync.dma_start(out=w1_raw[g][:], in_=w1_rows[:, :, PASS * g : PASS * (g + 1)])
 
         def load_w3(g):
-            w3_raw[g] = keep.tile([P, PACK, N], F32, name="w3_raw%d" % g, tag=("slot_t", "slot_a")[g], align_bytes=64)
+            w3_raw[g] = keep.tile([P, PACK, N], F32, name="w3_raw%d" % g, tag=("slot_s", "slot_t")[g], align_bytes=64)
             nc.sync.dma_start(out=w3_raw[g][:],
                               in_=w3[PASS * g : PASS * (g + 1), :].rearrange("(p j) n -> p j n", j=PACK))
 
         def load_w4():
-            w4_w[0] = keep.tile([P, GROUPS, N], I32, name="w4_w", tag="slot_s", align_bytes=64)
+            w4_w[0] = keep.tile([P, GROUPS, N], I32, name="w4_w", tag="slot_a", align_bytes=64)
             nc.sync.dma_start(out=w4_w[0][:], in_=w4_words.rearrange("g p n t -> p g (n t)").bitcast(I32))
 
-        def load_base(half):
-            base_sb[half] = keep.tile([P, N // P, HALF], F32, name="base%d" % half, tag=("slot_b", "slot_t")[half],
-                                      align_bytes=64)
-            nc.sync.dma_start(out=base_sb[half][:], in_=base_rows[:, :, HALF * half : HALF * (half + 1)])
+        def load_base():
+            base_sb[0] = keep.tile([P, N // P, S], F32, name="base_sb", tag="slot_b", align_bytes=64)
+            for u in range(2):
+                nc.sync.dma_start(out=base_sb[0][:, 2 * u : 2 * u + 2, :], in_=base_rows[:, 2 * u : 2 * u + 2, :])
 
         v_s = [keep.tile([P, HALF], U8, name="v_s%d" % half, align_bytes=64) for half in range(2)]
         v_w = [keep.tile([P, HALF], U32, name="v_w%d" % half, align_bytes=64) for half in range(2)]
@@ -122,15 +120,13 @@ def tile_list_book_impact_kernel(tc, tab_words, tab_scales, offs, w1, w2_words, 
         w1_s = [keep.tile([P, PASS], U8, name="w1_s%d" % g, align_bytes=64) for g in range(GROUPS)]
         w1_b = [keep.tile([P, PACK * PASS], BF16, name="w1_b%d" % g, align_bytes=64) for g in range(GROUPS)]
 
-        def round_w1(g):
-            dealt = w1_b[g][:].rearrange("p (t m j) -> p m t j", t=PACK, j=PACK)
-            for u in range(2):
-                raw = w1_raw[g][:, u].rearrange("p j (m t) -> p m t j", t=PACK)
-                if W1_ROUND[g][u] == "v":
-                    nc.vector.tensor_copy(dealt[:, 64 * u : 64 * (u + 1)], raw)
-                else:
-                    for m in range(0, 64, 32):
-                        nc.scalar.copy(dealt[:, 64 * u + m : 64 * u + m + 32], raw[:, m : m + 32])
+        def round_w1(g, engine, m0, m1):
+            dealt = w1_b[g][:].rearrange("p (t m j) -> p m t j", t=PACK, j=PACK)[:, m0:m1]
+            raw = w1_raw[g][:].rearrange("p j (m t) -> p m t j", t=PACK)[:, m0:m1]
+            if engine == "v":
+                nc.vector.tensor_copy(dealt, raw)
+            else:
+                nc.scalar.copy(dealt, raw)
 
         def quantise_w1(g):
             nc.vector.quantize_mx(out=w1_q[g][:].bitcast(FP8X4), scales=w1_s[g][:], in_=w1_b[g][:])
@@ -139,44 +135,43 @@ def tile_list_book_impact_kernel(tc, tab_words, tab_scales, offs, w1, w2_words, 
         w3_s = [keep.tile([P, N], U8, name="w3_s%d" % g, align_bytes=64) for g in range(GROUPS)]
         w3_b = [keep.tile([P, N, PACK], BF16, name="w3_b%d" % g, align_bytes=64) for g in range(GROUPS)]
 
-        def pool_round(dst, src, width):
-            for c in range(0, width, POOL_PIECE):
-                nc.gpsimd.tensor_scalar(dst[:, c : c + POOL_PIECE, :],
-                                        src[:, :, c : c + POOL_PIECE].rearrange("p j n -> p n j"),
-                                        1.0, 0.0, ALU.mult, ALU.add)
+        later = {}
 
-        def round_on(engine, dst, src, width):
-            if engine == "g":
-                pool_round(dst, src, width)
-            elif engine == "s":
-                for c in range(0, width, 128):
-                    nc.scalar.copy(dst[:, c : c + 128, :], src[:, :, c : c + 128].rearrange("p j n -> p n j"))
+        def at(step, work, *args):
+            later.setdefault(step, []).append((work, args))
+
+        def weave(engine, dst, src, c0, c1):
+            dst_v = dst[:, c0:c1, :].rearrange("p (c i) t -> p c t i", i=2)
+            src_v = src[:, :, c0:c1].rearrange("p t (c i) -> p c t i", i=2)
+            if engine == "v":
+                nc.vector.tensor_copy(dst_v, src_v)
             else:
-                nc.vector.tensor_copy(dst[:], src[:].rearrange("p t s -> p s t"))
+                nc.scalar.copy(dst_v, src_v)
 
-        def round_w3(g):
-            round_on(W3_ROUND[g], w3_b[g], w3_raw[g], N)
+        def round_on(step, engine, dst, src, width):
+            if engine == "v":
+                at(step, weave, engine, dst, src, 0, width)
+                return step
+            for i, c in enumerate(range(0, width, 128)):
+                at(step + i // 2, weave, engine, dst, src, c, c + 128)
+            return step + (width // 128 - 1) // 2
 
         def quantise_w3(g):
             nc.vector.quantize_mx(out=w3_q[g][:].bitcast(FP8X4), scales=w3_s[g][:],
                                   in_=w3_b[g][:].rearrange("p n j -> p (n j)"))
 
         h_s = keep.tile([P, GROUPS * S], U8, name="h_s", align_bytes=64)
+        h_q = keep.tile([P, GROUPS * S], U32, name="h_q", align_bytes=64)
 
         y_rows = out_0.rearrange("(i p) s -> p i s", p=P)
-        later = {}
-
-        def at(step, work, *args):
-            later.setdefault(step, []).append((work, args))
-
         def moving_v(c0, width):
             half, v0 = divmod(c0, HALF)
             return v_w[half][:, v0 : v0 + width].bitcast(FP8X4), v_s[half][:, v0 : v0 + width]
 
-        def saturate(c0, width, g, t0):
+        def square_a(c0, width, g, t0):
             v_words, v_scales = moving_v(c0, width)
             per_bank = BANK // width
-            a = psum.tile([P, per_bank, width], F32, name="a", bufs=3)
+            a = psum.tile([P, per_bank, width], F32, name="a", tag="a", bufs=4)
             for i in range(per_bank):
                 t = t0 + i
                 nc.tensor.matmul_mx(out=a[:, i, :], lhsT=w1_q[g][:, P * t : P * (t + 1)].bitcast(FP8X4),
@@ -184,6 +179,10 @@ def tile_list_book_impact_kernel(tc, tab_words, tab_scales, offs, w1, w2_words, 
                                     rhs=v_words, rhs_scale=v_scales, start=True, stop=True)
             square = ring.tile([P, per_bank, width], F32, name="square")
             nc.scalar.activation(square[:], a[:], ACT.Square)
+            return a, square
+
+        def saturate(step, c0, width, g, t0, a, square, h):
+            per_bank = BANK // width
             root = ring.tile([P, per_bank, width], F32, name="root")
             nc.scalar.activation(root[:], square[:], ACT.Abs_reciprocal_sqrt, bias=one[:])
             sat = ring.tile([P, per_bank, width], F32, name="sat")
@@ -191,7 +190,7 @@ def tile_list_book_impact_kernel(tc, tab_words, tab_scales, offs, w1, w2_words, 
                 t = t0 + i
                 nc.vector.scalar_tensor_tensor(sat[:, i, :], a[:, i, :], gain_s[:, g, t : t + 1], root[:, i, :],
                                                ALU.mult, ALU.mult)
-            return sat
+            at(step + 1, add_linear, c0, width, g, t0, sat, h)
 
         def add_linear(c0, width, g, t0, sat, h):
             v_words, v_scales = moving_v(c0, width)
@@ -208,48 +207,92 @@ def tile_list_book_impact_kernel(tc, tab_words, tab_scales, offs, w1, w2_words, 
                     out=out_1[PASS * g : PASS * (g + 1), c0 : c0 + width].rearrange("(p t) s -> p t s", t=PACK),
                     in_=h[:])
 
-        def quantise_h(c0, width, g, h_b, h_q):
-            nc.vector.quantize_mx(out=h_q[:, g, :].bitcast(FP8X4), scales=h_s[:, S * g + c0 : S * g + c0 + width],
+        def store_scales(c0, c1):
+            for q in range(4):
+                nc.sync.dma_start(
+                    out=out_3[:, 4 * q : 4 * q + 4, c0:c1].rearrange("g r m -> r g m").bitcast(I32),
+                    in_=h_s[32 * q : 32 * q + 4, :].rearrange("r (g m) -> r g m", g=GROUPS)[:, :, c0:c1].bitcast(I32))
+
+        def quantise_h(c0, width, g, h_b):
+            nc.vector.quantize_mx(out=h_q[:, S * g + c0 : S * g + c0 + width].bitcast(FP8X4), scales=h_s[:, S * g + c0 : S * g + c0 + width],
                                   in_=h_b[:].rearrange("p s t -> p (s t)"))
             if g == GROUPS - 1:
                 nc.sync.dma_start(
                     out=out_2[:, :, c0 : c0 + width, :].rearrange("g p m t -> p g (m t)").bitcast(I32),
-                    in_=h_q[:].bitcast(I32))
+                    in_=h_q[:].bitcast(I32).rearrange("p (g m) -> p g m", g=GROUPS)[:, :, c0 : c0 + width])
+                if c0 + width in SCALE_STORES:
+                    store_scales(SCALE_STORES[c0 + width], c0 + width)
 
-        def round_h(step, n, c0, width, g, h, h_q):
+        def round_h(step, n, c0, width, g, h):
             h_b = ring.tile([P, width, PACK], BF16, name="h_b", align_bytes=64)
-            round_on(H_ROUND[n][g], h_b, h, width)
-            at(step + 1, quantise_h, c0, width, g, h_b, h_q)
+            done = round_on(step + 1, H_ROUND[n], h_b, h, width)
+            at(done + 1, quantise_h, c0, width, g, h_b)
+            if c0 + width == S:
+                at(done + 2, last_readings, g, n, c0, width)
+            elif g == GROUPS - 1:
+                y = keep.tile([P, N // P, width], F32, name="y_%d" % c0)
+                for m, i0 in enumerate(range(0, N // P, BANK // width)):
+                    at(done + 2 + m, readings, done + 2 + m, n, c0, width, i0, y)
 
-        def readings(step, n, c0, width, i0, h_q, y):
+        def reading_passes(bank, words, scales, c0, width, i0, count, groups, one_group):
+            order = [(i, g) for i in range(count) for g in groups]
+            for i, g in order:
+                cols = slice(P * (i0 + i), P * (i0 + i + 1))
+                first = g == 0 and (i == 0 or not one_group)
+                last = g == GROUPS - 1 and (i == count - 1 or not one_group)
+                nc.tensor.matmul_mx(out=bank[:, i, :], lhsT=words[g][:, cols].bitcast(FP8X4),
+                                    lhsT_scale=scales[g][:, cols], rhs=h_q[:, S * g + c0 : S * g + c0 + width].bitcast(FP8X4),
+                                    rhs_scale=h_s[:, S * g + c0 : S * g + c0 + width], start=first, stop=last)
+
+        def weights_of_readings():
+            return (([w3_q[g][:] for g in range(GROUPS)], [w3_s[g][:] for g in range(GROUPS)]),
+                    ([w4_w[0][:, g, :] for g in range(GROUPS)], [w4_s[:, g, :] for g in range(GROUPS)]))
+
+        def multiply(d, e, count, width):
+            d_sb = ring.tile([P, count, width], F32, name="d_sb")
+            nc.scalar.copy(d_sb[:], d[:])
+            prod = ring.tile([P, count, width], F32, name="prod")
+            nc.vector.tensor_tensor(prod[:], d_sb[:], e[:], ALU.mult)
+            return prod
+
+        def readings(step, n, c0, width, i0, y):
             per_bank = BANK // width
             d = psum.tile([P, per_bank, width], F32, name="d", bufs=1)
-            e = psum.tile([P, per_bank, width], F32, name="e", bufs=2)
-            for bank, words, scales in ((d, [w3_q[g][:] for g in range(GROUPS)], [w3_s[g][:] for g in range(GROUPS)]),
-                                        (e, [w4_w[0][:, g, :] for g in range(GROUPS)], [w4_s[:, g, :] for g in range(GROUPS)])):
-                for i in range(per_bank):
-                    cols = slice(P * (i0 + i), P * (i0 + i + 1))
-                    for g in range(GROUPS):
-                        nc.tensor.matmul_mx(out=bank[:, i, :], lhsT=words[g][:, cols].bitcast(FP8X4),
-                                            lhsT_scale=scales[g][:, cols], rhs=h_q[:, g, :].bitcast(FP8X4),
-                                            rhs_scale=h_s[:, S * g + c0 : S * g + c0 + width],
-                                            start=(g == 0), stop=(g == GROUPS - 1))
-            d_sb = ring.tile([P, per_bank, width], F32, name="d_sb")
-            nc.scalar.copy(d_sb[:], d[:])
-            prod = ring.tile([P, per_bank, width], F32, name="prod")
-            nc.vector.tensor_tensor(prod[:], d_sb[:], e[:], ALU.mult)
-            at(step + 1, less_base, n, c0, width, i0, prod, y)
+            e = psum.tile([P, per_bank, width], F32, name="e", bufs=1)
+            for bank, (words, scales) in zip((d, e), weights_of_readings()):
+                reading_passes(bank, words, scales, c0, width, i0, per_bank, range(GROUPS), False)
+            at(step + 1, less_base, n, c0, width, i0, per_bank, multiply(d, e, per_bank, width), y)
 
-        def less_base(n, c0, width, i0, prod, y):
-            half, v0 = divmod(c0, HALF)
-            per_bank = BANK // width
-            rows = slice(i0, i0 + per_bank)
+        last_banks = {}
+
+        def last_readings(g, n, c0, width):
+            for i0 in (0, 2):
+                for r, (words, scales) in enumerate(weights_of_readings()):
+                    if g == 0:
+                        last_banks[i0, r] = psum.tile([P, 2, width], F32, name="last_%d_%d" % (i0, r), tag="a", bufs=4)
+                    reading_passes(last_banks[i0, r], words, scales, c0, width, i0, 2, [g], True)
+            if g == GROUPS - 1:
+                y = keep.tile([P, N // P, width], F32, name="y_%d" % c0)
+                prods = [multiply(last_banks[i0, 0], last_banks[i0, 1], 2, width) for i0 in (0, 2)]
+                for i0, prod in zip((0, 2), prods):
+                    less_base(n, c0, width, i0, 2, prod, y)
+
+        def less_base(n, c0, width, i0, count, prod, y):
+            rows = slice(i0, i0 + count)
             engine = nc.gpsimd if SUB[n] == "g" else nc.vector
-            engine.tensor_tensor(y[:, rows, :], prod[:], base_sb[half][:, rows, v0 : v0 + width], ALU.subtract)
-            done = i0 + per_bank
+            engine.tensor_tensor(y[:, rows, :], prod[:], base_sb[0][:, rows, c0 : c0 + width], ALU.subtract)
+            done = i0 + count
             if done % 2 == 0:
-                first = max(0, done - max(2, per_bank))
+                first = max(0, done - max(2, count))
                 nc.sync.dma_start(out=y_rows[:, first:done, c0 : c0 + width], in_=y[:, first:done, :])
+
+        def prepare_w3(step, g):
+            done = round_on(step, W3_ROUND[g], w3_b[g], w3_raw[g], N)
+            at(done + 1, quantise_w3, g)
+
+        def tick(step):
+            for work, args in later.pop(step, []):
+                work(*args)
 
         deal_w2_words(0)
         deal_w2_words(1)
@@ -257,46 +300,30 @@ def tile_list_book_impact_kernel(tc, tab_words, tab_scales, offs, w1, w2_words, 
         load_w1(1)
         gather_scales(0)
         gather_scales(1)
-        load_w4()
+        load_w3(0)
         gather_words(0)
-        round_w1(0)
+        round_w1(0, "s", 0, 40)
+        round_w1(0, "v", 40, 128)
+        load_w4()
         quantise_w1(0)
         deal_w2_scales(0)
         gather_words(1)
         deal_w2_scales(1)
-        load_w3(0)
         load_w3(1)
-        at(1, round_w1, 1)
-        at(2, quantise_w1, 1)
-        at(2, load_base, 0)
-        at(3, round_w3, 0)
-        at(4, quantise_w3, 0)
-        at(4, load_base, 1)
-        at(5, round_w3, 1)
-        at(7, quantise_w3, 1)
+        for i in range(4):
+            at(1 + i // 2, round_w1, 1, "s", 32 * i, 32 * (i + 1))
+        at(3, quantise_w1, 1)
+        at(3, load_base)
+        prepare_w3(3, 0)
+        prepare_w3(5, 1)
         step = 0
-
-        def tick(step):
-            for work, args in later.pop(step, []):
-                work(*args)
-
-        for n, (c0, width) in enumerate(CHUNKS):
-            per_bank = BANK // width
-            h_q = keep.tile([P, GROUPS, width], U32, name="h_q%d" % c0, align_bytes=64)
-            y = keep.tile([P, N // P, width], F32, name="y_%d" % c0)
-            for g in range(GROUPS):
-                h = keep.tile([P, PACK, width], F32, name="h_%d_%d" % (c0, g))
-                for t0 in range(0, PACK, per_bank):
-                    sat = saturate(c0, width, g, t0)
-                    at(step + 1, add_linear, c0, width, g, t0, sat, h)
-                    tick(step)
-                    step = step + 1
-                at(step + 1, round_h, step + 1, n, c0, width, g, h, h_q)
-            for m, i0 in enumerate(range(0, N // P, per_bank)):
-                at(step + 3 + m, readings, step + 3 + m, n, c0, width, i0, h_q, y)
-        for tail in range(step, step + 8):
+        for n, (c0, width, g) in enumerate(BLOCKS):
+            h = keep.tile([P, PACK, width], F32, name="h_%d_%d" % (c0, g))
+            for t0 in range(0, PACK, BANK // width):
+                a, square = square_a(c0, width, g, t0)
+                at(step + 1, saturate, step + 1, c0, width, g, t0, a, square, h)
+                tick(step)
+                step = step + 1
+            at(step + 1, round_h, step + 1, n, c0, width, g, h)
+        for tail in range(step, step + 10):
             tick(tail)
-        for q in range(4):
-            nc.sync.dma_start(
-                out=out_3[:, 4 * q : 4 * q + 4, :].rearrange("g r m -> r g m").bitcast(I32),
-                in_=h_s[32 * q : 32 * q + 4, :].bitcast(I32).rearrange("r (g m) -> r g m", g=GROUPS))

@@ -21,13 +21,16 @@ PACK = 4
 PASS = P * PACK
 BANK = 512
 GROUPS = H // PASS
-HALF = 512
-BLOCKS = [(0, 512, 0), (0, 256, 1), (256, 256, 1), (512, 256, 0), (512, 256, 1), (768, 128, 0), (768, 128, 1), (896, 128, 0), (896, 128, 1)]
-POOL_PIECE = 128
-H_ROUND = "sssssssvv"
-SUB = "vvvvvvvvv"
-W3_ROUND = "vv"
-SCALE_STORES = {768: 0, 1024: 768}
+QUADRANTS = 4
+HALF = S // 2
+LIST_COLS = HALF // 16
+
+BLOCKS = [(0, 512, 0), (0, 256, 1), (256, 256, 1), (512, 256, 0), (512, 256, 1),
+          (768, 128, 0), (768, 128, 1), (896, 128, 0), (896, 128, 1)]
+LAST = S - BLOCKS[-1][1]
+SCALAR_PIECE = 128
+EARLY = 768
+TAIL_STEPS = 10
 
 
 def tile_list_book_impact_kernel(tc, tab_words, tab_scales, offs, w1, w2_words, w2_scales, gain,
@@ -44,132 +47,137 @@ def tile_list_book_impact_kernel(tc, tab_words, tab_scales, offs, w1, w2_words, 
         w2_w = []
         for g in range(GROUPS):
             words = keep.tile([P, 2 * PASS], U8, name="w2_w%d" % g, tag=("slot_a", "slot_b")[g], align_bytes=64)
-            nc.sync.dma_start(out=words[:].bitcast(I32), in_=w2_words[0, :, 2 * PASS * g : 2 * PASS * (g + 1)].bitcast(I32))
+            nc.sync.dma_start(out=words[:].bitcast(I32),
+                              in_=w2_words[0, :, 2 * PASS * g : 2 * PASS * (g + 1)].bitcast(I32))
             w2_w.append(words)
-        tab_w = keep.tile([P, T], I32, name="tab_w", tag="slot_t", align_bytes=64)
-        nc.sync.dma_start(out=tab_w[:], in_=tab_words[0].rearrange("p n t -> p (n t)").bitcast(I32))
-        tab_s = keep.tile([P, T], U8, name="tab_s", tag="slot_s", align_bytes=64)
-        nc.vector.memset(tab_s[:].bitcast(I32), 0)
-        for q in range(4):
-            nc.scalar.dma_start(out=tab_s[32 * q : 32 * q + 4, :].bitcast(I32),
-                                in_=tab_scales[0, 4 * q : 4 * q + 4, :].bitcast(I32))
 
-        w2_s = keep.tile([P, H], U8, name="w2_s", align_bytes=64)
-        nc.vector.memset(w2_s[:].bitcast(I32), 0)
-        for q in range(4):
-            nc.scalar.dma_start(out=w2_s[32 * q : 32 * q + 4, :].bitcast(I32),
-                                in_=w2_scales[0, 4 * q : 4 * q + 4, :].bitcast(I32))
+        def load_scale_rows(plane, rows):
+            nc.vector.memset(plane[:].bitcast(I32), 0)
+            for q in range(QUADRANTS):
+                nc.scalar.dma_start(out=plane[32 * q : 32 * q + 4, :].bitcast(I32),
+                                    in_=rows[4 * q : 4 * q + 4, :].bitcast(I32))
+
+        tab_s = keep.tile([P, T], U8, name="tab_s", tag="slot_s", align_bytes=64)
+        load_scale_rows(tab_s, tab_scales[0])
 
         one = keep.tile([P, 1], F32, name="one")
-        nc.gpsimd.memset(one[:], 1.0)
+        nc.vector.memset(one[:], 1.0)
         warm = keep.tile([P, 1], F32, name="warm")
         nc.scalar.activation(warm[:], one[:], ACT.Abs_reciprocal_sqrt)
 
-        gain_s = keep.tile([P, GROUPS, PACK], F32, name="gain_s")
-        nc.gpsimd.dma_start(out=gain_s[:], in_=gain.rearrange("(g p t) -> p g t", g=GROUPS, t=PACK))
-        w4_s = keep.tile([P, GROUPS, N], U8, name="w4_s", align_bytes=64)
-        for q in range(4):
-            nc.gpsimd.dma_start(out=w4_s[32 * q : 32 * q + 4, :, :].bitcast(I32),
-                                in_=w4_scales[:, 4 * q : 4 * q + 4, :].rearrange("g r n -> r g n").bitcast(I32))
+        w2_s = keep.tile([P, H], U8, name="w2_s", tag="slot_w", align_bytes=64)
+        load_scale_rows(w2_s, w2_scales[0])
 
-        w1_rows = w1.rearrange("(p j) c -> p j c", j=PACK)
-        base_rows = base.rearrange("(i p) s -> p i s", p=P)
-        w1_raw, w3_raw, base_sb, w4_w = {}, {}, {}, {}
+        gain_sb = keep.tile([P, GROUPS, PACK], F32, name="gain_sb")
+        loaded = {}
+
+        def load_table():
+            loaded["tab"] = keep.tile([P, T], I32, name="tab_w", tag="slot_a", align_bytes=64)
+            nc.sync.dma_start(out=loaded["tab"][:], in_=tab_words[0].rearrange("p n t -> p (n t)").bitcast(I32))
 
         def load_w1(g):
-            w1_raw[g] = keep.tile([P, PACK, PASS], F32, name="w1_raw%d" % g, tag=("slot_a", "slot_b")[g], align_bytes=64)
-            nc.sync.dma_start(out=w1_raw[g][:], in_=w1_rows[:, :, PASS * g : PASS * (g + 1)])
+            loaded["w1", g] = keep.tile([P, PACK, PASS], F32, name="w1_raw%d" % g, tag=("slot_c", "slot_b")[g],
+                                        align_bytes=64)
+            nc.sync.dma_start(out=loaded["w1", g][:],
+                              in_=w1.rearrange("(p j) c -> p j c", j=PACK)[:, :, PASS * g : PASS * (g + 1)])
 
         def load_w3(g):
-            w3_raw[g] = keep.tile([P, PACK, N], F32, name="w3_raw%d" % g, tag=("slot_s", "slot_t")[g], align_bytes=64)
-            nc.sync.dma_start(out=w3_raw[g][:],
+            loaded["w3", g] = keep.tile([P, PACK, N], F32, name="w3_raw%d" % g, tag=("slot_s", "slot_a")[g],
+                                        align_bytes=64)
+            nc.sync.dma_start(out=loaded["w3", g][:],
                               in_=w3[PASS * g : PASS * (g + 1), :].rearrange("(p j) n -> p j n", j=PACK))
 
-        def load_w4():
-            w4_w[0] = keep.tile([P, GROUPS, N], I32, name="w4_w", tag="slot_a", align_bytes=64)
-            nc.sync.dma_start(out=w4_w[0][:], in_=w4_words.rearrange("g p n t -> p g (n t)").bitcast(I32))
+        def load_w4_words():
+            loaded["w4_w"] = keep.tile([P, GROUPS, N], I32, name="w4_w", tag="slot_c", align_bytes=64)
+            nc.sync.dma_start(out=loaded["w4_w"][:], in_=w4_words.rearrange("g p n t -> p g (n t)").bitcast(I32))
+
+        def load_w4_scales():
+            loaded["w4_s"] = keep.tile([P, GROUPS, N], U8, name="w4_s", tag="slot_w", align_bytes=64)
+            for q in range(QUADRANTS):
+                nc.sync.dma_start(out=loaded["w4_s"][32 * q : 32 * q + 4, :, :].bitcast(I32),
+                                  in_=w4_scales[:, 4 * q : 4 * q + 4, :].rearrange("g r n -> r g n").bitcast(I32))
 
         def load_base():
-            base_sb[0] = keep.tile([P, N // P, S], F32, name="base_sb", tag="slot_b", align_bytes=64)
-            for u in range(2):
-                nc.sync.dma_start(out=base_sb[0][:, 2 * u : 2 * u + 2, :], in_=base_rows[:, 2 * u : 2 * u + 2, :])
+            loaded["base"] = keep.tile([P, N // P, S], F32, name="base_sb", tag="slot_b", align_bytes=64)
+            base_rows = base.rearrange("(i p) s -> p i s", p=P)
+            for i0 in (0, 2):
+                nc.sync.dma_start(out=loaded["base"][:, i0 : i0 + 2, :], in_=base_rows[:, i0 : i0 + 2, :])
 
         v_s = [keep.tile([P, HALF], U8, name="v_s%d" % half, align_bytes=64) for half in range(2)]
         v_w = [keep.tile([P, HALF], U32, name="v_w%d" % half, align_bytes=64) for half in range(2)]
 
         def gather_scales(half):
-            nc.vector.tensor_copy(v_s[half][:], tab_s[:].indirect(offsets[:, 32 * half : 32 * (half + 1)]))
+            entries = offsets[:, LIST_COLS * half : LIST_COLS * (half + 1)]
+            nc.vector.tensor_copy(v_s[half][:], tab_s[:].indirect(entries))
 
         def gather_words(half):
-            nc.vector.tensor_copy(v_w[half][:], tab_w[:].bitcast(U32).indirect(offsets[:, 32 * half : 32 * (half + 1)]))
+            entries = offsets[:, LIST_COLS * half : LIST_COLS * (half + 1)]
+            nc.vector.tensor_copy(v_w[half][:], loaded["tab"][:].bitcast(U32).indirect(entries))
 
-        w2_wp = [keep.tile([P, 2 * PASS], U8, name="w2_wp%d" % g, align_bytes=64) for g in range(GROUPS)]
-        w2_sp = [keep.tile([P, PASS], U8, name="w2_sp%d" % g, align_bytes=64) for g in range(GROUPS)]
+        def looked_up(c0, width):
+            half, v0 = divmod(c0, HALF)
+            return v_w[half][:, v0 : v0 + width].bitcast(FP8X4), v_s[half][:, v0 : v0 + width]
+
+        w2_wd = [keep.tile([P, 2 * PASS], U8, name="w2_wd%d" % g, align_bytes=64) for g in range(GROUPS)]
+        w2_sd = [keep.tile([P, PASS], U8, name="w2_sd%d" % g, align_bytes=64) for g in range(GROUPS)]
 
         def deal_w2_words(g):
-            nc.vector.tensor_copy(
-                w2_wp[g][:].bitcast(U16).rearrange("p (t m) -> p t m", t=PACK),
-                w2_w[g][:].bitcast(U16).rearrange("p (m t) -> p t m", t=PACK))
+            nc.vector.tensor_copy(w2_wd[g][:].bitcast(U16).rearrange("p (t m) -> p t m", t=PACK),
+                                  w2_w[g][:].bitcast(U16).rearrange("p (m t) -> p t m", t=PACK))
 
         def deal_w2_scales(g):
-            nc.vector.tensor_copy(
-                w2_sp[g][:].rearrange("p (t m) -> p t m", t=PACK),
-                w2_s[:, PASS * g : PASS * (g + 1)].rearrange("p (m t) -> p t m", t=PACK))
+            nc.vector.tensor_copy(w2_sd[g][:].rearrange("p (t m) -> p t m", t=PACK),
+                                  w2_s[:, PASS * g : PASS * (g + 1)].rearrange("p (m t) -> p t m", t=PACK))
 
         w1_q = [keep.tile([P, PASS], U32, name="w1_q%d" % g, align_bytes=64) for g in range(GROUPS)]
         w1_s = [keep.tile([P, PASS], U8, name="w1_s%d" % g, align_bytes=64) for g in range(GROUPS)]
         w1_b = [keep.tile([P, PACK * PASS], BF16, name="w1_b%d" % g, align_bytes=64) for g in range(GROUPS)]
 
-        def round_w1(g, engine, m0, m1):
-            dealt = w1_b[g][:].rearrange("p (t m j) -> p m t j", t=PACK, j=PACK)[:, m0:m1]
-            raw = w1_raw[g][:].rearrange("p j (m t) -> p m t j", t=PACK)[:, m0:m1]
-            if engine == "v":
-                nc.vector.tensor_copy(dealt, raw)
-            else:
-                nc.scalar.copy(dealt, raw)
+        def round_w1(copy, g, m0, m1):
+            copy(w1_b[g][:].rearrange("p (t m j) -> p m t j", t=PACK, j=PACK)[:, m0:m1],
+                 loaded["w1", g][:].rearrange("p j (m t) -> p m t j", t=PACK)[:, m0:m1])
 
         def quantise_w1(g):
             nc.vector.quantize_mx(out=w1_q[g][:].bitcast(FP8X4), scales=w1_s[g][:], in_=w1_b[g][:])
 
+        def weave(copy, dst, src, c0, c1):
+            copy(dst[:, c0:c1, :].rearrange("p (c i) t -> p c t i", i=2),
+                 src[:, :, c0:c1].rearrange("p t (c i) -> p c t i", i=2))
+
         w3_q = [keep.tile([P, N], U32, name="w3_q%d" % g, align_bytes=64) for g in range(GROUPS)]
         w3_s = [keep.tile([P, N], U8, name="w3_s%d" % g, align_bytes=64) for g in range(GROUPS)]
         w3_b = [keep.tile([P, N, PACK], BF16, name="w3_b%d" % g, align_bytes=64) for g in range(GROUPS)]
+
+        def round_w3(g):
+            weave(nc.vector.tensor_copy, w3_b[g], loaded["w3", g], 0, N)
+
+        def quantise_w3(g):
+            nc.vector.quantize_mx(out=w3_q[g][:].bitcast(FP8X4), scales=w3_s[g][:],
+                                  in_=w3_b[g][:].rearrange("p n j -> p (n j)"))
 
         later = {}
 
         def at(step, work, *args):
             later.setdefault(step, []).append((work, args))
 
-        def weave(engine, dst, src, c0, c1):
-            dst_v = dst[:, c0:c1, :].rearrange("p (c i) t -> p c t i", i=2)
-            src_v = src[:, :, c0:c1].rearrange("p t (c i) -> p c t i", i=2)
-            if engine == "v":
-                nc.vector.tensor_copy(dst_v, src_v)
-            else:
-                nc.scalar.copy(dst_v, src_v)
+        def tick(step):
+            for work, args in later.pop(step, []):
+                work(*args)
 
-        def round_on(step, engine, dst, src, width):
-            if engine == "v":
-                at(step, weave, engine, dst, src, 0, width)
-                return step
-            for i, c in enumerate(range(0, width, 128)):
-                at(step + i // 2, weave, engine, dst, src, c, c + 128)
-            return step + (width // 128 - 1) // 2
-
-        def quantise_w3(g):
-            nc.vector.quantize_mx(out=w3_q[g][:].bitcast(FP8X4), scales=w3_s[g][:],
-                                  in_=w3_b[g][:].rearrange("p n j -> p (n j)"))
-
-        h_s = keep.tile([P, GROUPS * S], U8, name="h_s", align_bytes=64)
         h_q = keep.tile([P, GROUPS * S], U32, name="h_q", align_bytes=64)
+        h_s_early = keep.tile([P, GROUPS, EARLY], U8, name="h_s_early", align_bytes=64)
+        h_s_late = keep.tile([P, GROUPS, S - EARLY], U8, name="h_s_late", align_bytes=64)
 
-        y_rows = out_0.rearrange("(i p) s -> p i s", p=P)
-        def moving_v(c0, width):
-            half, v0 = divmod(c0, HALF)
-            return v_w[half][:, v0 : v0 + width].bitcast(FP8X4), v_s[half][:, v0 : v0 + width]
+        def h_words(c0, width, g):
+            return h_q[:, S * g + c0 : S * g + c0 + width]
+
+        def h_scales(c0, width, g):
+            if c0 < EARLY:
+                return h_s_early[:, g, c0 : c0 + width]
+            return h_s_late[:, g, c0 - EARLY : c0 - EARLY + width]
 
         def square_a(c0, width, g, t0):
-            v_words, v_scales = moving_v(c0, width)
+            v_words, v_scales = looked_up(c0, width)
             per_bank = BANK // width
             a = psum.tile([P, per_bank, width], F32, name="a", tag="a", bufs=4)
             for i in range(per_bank):
@@ -188,18 +196,18 @@ def tile_list_book_impact_kernel(tc, tab_words, tab_scales, offs, w1, w2_words, 
             sat = ring.tile([P, per_bank, width], F32, name="sat")
             for i in range(per_bank):
                 t = t0 + i
-                nc.vector.scalar_tensor_tensor(sat[:, i, :], a[:, i, :], gain_s[:, g, t : t + 1], root[:, i, :],
+                nc.vector.scalar_tensor_tensor(sat[:, i, :], a[:, i, :], gain_sb[:, g, t : t + 1], root[:, i, :],
                                                ALU.mult, ALU.mult)
             at(step + 1, add_linear, c0, width, g, t0, sat, h)
 
         def add_linear(c0, width, g, t0, sat, h):
-            v_words, v_scales = moving_v(c0, width)
+            v_words, v_scales = looked_up(c0, width)
             per_bank = BANK // width
             b = psum.tile([P, per_bank, width], F32, name="b", bufs=2)
             for i in range(per_bank):
                 t = t0 + i
-                nc.tensor.matmul_mx(out=b[:, i, :], lhsT=w2_wp[g][:, 2 * P * t : 2 * P * (t + 1)].bitcast(FP4X4),
-                                    lhsT_scale=w2_sp[g][:, P * t : P * (t + 1)],
+                nc.tensor.matmul_mx(out=b[:, i, :], lhsT=w2_wd[g][:, 2 * P * t : 2 * P * (t + 1)].bitcast(FP4X4),
+                                    lhsT_scale=w2_sd[g][:, P * t : P * (t + 1)],
                                     rhs=v_words, rhs_scale=v_scales, start=True, stop=True)
             nc.vector.tensor_tensor(h[:, t0 : t0 + per_bank, :], sat[:], b[:], ALU.add)
             if t0 + per_bank == PACK:
@@ -207,46 +215,48 @@ def tile_list_book_impact_kernel(tc, tab_words, tab_scales, offs, w1, w2_words, 
                     out=out_1[PASS * g : PASS * (g + 1), c0 : c0 + width].rearrange("(p t) s -> p t s", t=PACK),
                     in_=h[:])
 
-        def store_scales(c0, c1):
-            for q in range(4):
-                nc.sync.dma_start(
-                    out=out_3[:, 4 * q : 4 * q + 4, c0:c1].rearrange("g r m -> r g m").bitcast(I32),
-                    in_=h_s[32 * q : 32 * q + 4, :].rearrange("r (g m) -> r g m", g=GROUPS)[:, :, c0:c1].bitcast(I32))
+        def store_scales(plane, c0, c1):
+            for q in range(QUADRANTS):
+                nc.sync.dma_start(out=out_3[:, 4 * q : 4 * q + 4, c0:c1].rearrange("g r m -> r g m").bitcast(I32),
+                                  in_=plane[32 * q : 32 * q + 4, :, :].bitcast(I32))
 
         def quantise_h(c0, width, g, h_b):
-            nc.vector.quantize_mx(out=h_q[:, S * g + c0 : S * g + c0 + width].bitcast(FP8X4), scales=h_s[:, S * g + c0 : S * g + c0 + width],
+            nc.vector.quantize_mx(out=h_words(c0, width, g).bitcast(FP8X4), scales=h_scales(c0, width, g),
                                   in_=h_b[:].rearrange("p s t -> p (s t)"))
-            if g == GROUPS - 1:
-                nc.sync.dma_start(
-                    out=out_2[:, :, c0 : c0 + width, :].rearrange("g p m t -> p g (m t)").bitcast(I32),
-                    in_=h_q[:].bitcast(I32).rearrange("p (g m) -> p g m", g=GROUPS)[:, :, c0 : c0 + width])
-                if c0 + width in SCALE_STORES:
-                    store_scales(SCALE_STORES[c0 + width], c0 + width)
+            nc.sync.dma_start(out=out_2[g, :, c0 : c0 + width, :].rearrange("p m t -> p (m t)").bitcast(I32),
+                              in_=h_words(c0, width, g).bitcast(I32))
+            if g == GROUPS - 1 and c0 + width == EARLY:
+                store_scales(h_s_early, 0, EARLY)
+            if g == GROUPS - 1 and c0 + width == S:
+                store_scales(h_s_late, EARLY, S)
 
-        def round_h(step, n, c0, width, g, h):
+        def after_block(step, c0, width, g, h):
             h_b = ring.tile([P, width, PACK], BF16, name="h_b", align_bytes=64)
-            done = round_on(step + 1, H_ROUND[n], h_b, h, width)
-            at(done + 1, quantise_h, c0, width, g, h_b)
-            if c0 + width == S:
-                at(done + 2, last_readings, g, n, c0, width)
+            if c0 < LAST:
+                pieces = width // SCALAR_PIECE
+                for i in range(pieces):
+                    at(step + i // 2, weave, nc.scalar.copy, h_b, h, SCALAR_PIECE * i, SCALAR_PIECE * (i + 1))
+                rounded = step + (pieces - 1) // 2
+            else:
+                at(step, weave, nc.vector.tensor_copy, h_b, h, 0, width)
+                rounded = step
+            at(rounded + 1, quantise_h, c0, width, g, h_b)
+            if c0 == LAST:
+                at(rounded + 2, last_readings, g, c0, width)
             elif g == GROUPS - 1:
                 y = keep.tile([P, N // P, width], F32, name="y_%d" % c0)
                 for m, i0 in enumerate(range(0, N // P, BANK // width)):
-                    at(done + 2 + m, readings, done + 2 + m, n, c0, width, i0, y)
+                    at(rounded + 2 + m, readings, rounded + 2 + m, c0, width, i0, y)
 
-        def reading_passes(bank, words, scales, c0, width, i0, count, groups, one_group):
-            order = [(i, g) for i in range(count) for g in groups]
-            for i, g in order:
-                cols = slice(P * (i0 + i), P * (i0 + i + 1))
-                first = g == 0 and (i == 0 or not one_group)
-                last = g == GROUPS - 1 and (i == count - 1 or not one_group)
-                nc.tensor.matmul_mx(out=bank[:, i, :], lhsT=words[g][:, cols].bitcast(FP8X4),
-                                    lhsT_scale=scales[g][:, cols], rhs=h_q[:, S * g + c0 : S * g + c0 + width].bitcast(FP8X4),
-                                    rhs_scale=h_s[:, S * g + c0 : S * g + c0 + width], start=first, stop=last)
-
-        def weights_of_readings():
+        def reading_weights():
             return (([w3_q[g][:] for g in range(GROUPS)], [w3_s[g][:] for g in range(GROUPS)]),
-                    ([w4_w[0][:, g, :] for g in range(GROUPS)], [w4_s[:, g, :] for g in range(GROUPS)]))
+                    ([loaded["w4_w"][:, g, :] for g in range(GROUPS)], [loaded["w4_s"][:, g, :] for g in range(GROUPS)]))
+
+        def reading_pass(out, words, scales, i, c0, width, g, start, stop):
+            cols = slice(P * i, P * (i + 1))
+            nc.tensor.matmul_mx(out=out, lhsT=words[g][:, cols].bitcast(FP8X4), lhsT_scale=scales[g][:, cols],
+                                rhs=h_words(c0, width, g).bitcast(FP8X4), rhs_scale=h_scales(c0, width, g),
+                                start=start, stop=stop)
 
         def multiply(d, e, count, width):
             d_sb = ring.tile([P, count, width], F32, name="d_sb")
@@ -255,75 +265,77 @@ def tile_list_book_impact_kernel(tc, tab_words, tab_scales, offs, w1, w2_words, 
             nc.vector.tensor_tensor(prod[:], d_sb[:], e[:], ALU.mult)
             return prod
 
-        def readings(step, n, c0, width, i0, y):
+        def less_base(c0, width, i0, count, prod, y):
+            rows = slice(i0, i0 + count)
+            if c0 < EARLY:
+                for i in range(count):
+                    nc.gpsimd.tensor_tensor(y[:, i0 + i, :], prod[:, i, :], loaded["base"][:, i0 + i, c0 : c0 + width],
+                                            ALU.subtract)
+            else:
+                nc.vector.tensor_tensor(y[:, rows, :], prod[:], loaded["base"][:, rows, c0 : c0 + width], ALU.subtract)
+            nc.sync.dma_start(out=out_0.rearrange("(i p) s -> p i s", p=P)[:, rows, c0 : c0 + width], in_=y[:, rows, :])
+
+        def readings(step, c0, width, i0, y):
             per_bank = BANK // width
             d = psum.tile([P, per_bank, width], F32, name="d", bufs=1)
             e = psum.tile([P, per_bank, width], F32, name="e", bufs=1)
-            for bank, (words, scales) in zip((d, e), weights_of_readings()):
-                reading_passes(bank, words, scales, c0, width, i0, per_bank, range(GROUPS), False)
-            at(step + 1, less_base, n, c0, width, i0, per_bank, multiply(d, e, per_bank, width), y)
+            for bank, (words, scales) in zip((d, e), reading_weights()):
+                for i in range(per_bank):
+                    for g in range(GROUPS):
+                        reading_pass(bank[:, i, :], words, scales, i0 + i, c0, width, g, g == 0, g == GROUPS - 1)
+            at(step + 1, less_base, c0, width, i0, per_bank, multiply(d, e, per_bank, width), y)
 
         last_banks = {}
 
-        def last_readings(g, n, c0, width):
+        def last_readings(g, c0, width):
             for i0 in (0, 2):
-                for r, (words, scales) in enumerate(weights_of_readings()):
+                for r, (words, scales) in enumerate(reading_weights()):
                     if g == 0:
                         last_banks[i0, r] = psum.tile([P, 2, width], F32, name="last_%d_%d" % (i0, r), tag="a", bufs=4)
-                    reading_passes(last_banks[i0, r], words, scales, c0, width, i0, 2, [g], True)
+                    for i in range(2):
+                        reading_pass(last_banks[i0, r][:, i, :], words, scales, i0 + i, c0, width, g,
+                                     g == 0 and i == 0, g == GROUPS - 1 and i == 1)
             if g == GROUPS - 1:
                 y = keep.tile([P, N // P, width], F32, name="y_%d" % c0)
                 prods = [multiply(last_banks[i0, 0], last_banks[i0, 1], 2, width) for i0 in (0, 2)]
                 for i0, prod in zip((0, 2), prods):
-                    less_base(n, c0, width, i0, 2, prod, y)
+                    less_base(c0, width, i0, 2, prod, y)
 
-        def less_base(n, c0, width, i0, count, prod, y):
-            rows = slice(i0, i0 + count)
-            engine = nc.gpsimd if SUB[n] == "g" else nc.vector
-            engine.tensor_tensor(y[:, rows, :], prod[:], base_sb[0][:, rows, c0 : c0 + width], ALU.subtract)
-            done = i0 + count
-            if done % 2 == 0:
-                first = max(0, done - max(2, count))
-                nc.sync.dma_start(out=y_rows[:, first:done, c0 : c0 + width], in_=y[:, first:done, :])
-
-        def prepare_w3(step, g):
-            done = round_on(step, W3_ROUND[g], w3_b[g], w3_raw[g], N)
-            at(done + 1, quantise_w3, g)
-
-        def tick(step):
-            for work, args in later.pop(step, []):
-                work(*args)
-
-        deal_w2_words(0)
-        deal_w2_words(1)
         load_w1(0)
+        nc.sync.dma_start(out=gain_sb[:], in_=gain.rearrange("(g p t) -> p g t", g=GROUPS, t=PACK))
+        deal_w2_words(0)
+        load_table()
+        deal_w2_words(1)
         load_w1(1)
         gather_scales(0)
+        round_w1(nc.vector.tensor_copy, 0, 0, P)
         gather_scales(1)
-        load_w3(0)
-        gather_words(0)
-        round_w1(0, "s", 0, 40)
-        round_w1(0, "v", 40, 128)
-        load_w4()
         quantise_w1(0)
+        load_w3(0)
+        load_w4_words()
         deal_w2_scales(0)
-        gather_words(1)
         deal_w2_scales(1)
-        load_w3(1)
+        load_w4_scales()
+        gather_words(0)
+
+        at(0, gather_words, 1)
+        at(0, load_w3, 1)
         for i in range(4):
-            at(1 + i // 2, round_w1, 1, "s", 32 * i, 32 * (i + 1))
+            at(1 + i // 2, round_w1, nc.scalar.copy, 1, 32 * i, 32 * (i + 1))
         at(3, quantise_w1, 1)
         at(3, load_base)
-        prepare_w3(3, 0)
-        prepare_w3(5, 1)
+        for g in range(GROUPS):
+            at(3 + 2 * g, round_w3, g)
+            at(4 + 2 * g, quantise_w3, g)
+
         step = 0
-        for n, (c0, width, g) in enumerate(BLOCKS):
+        for c0, width, g in BLOCKS:
             h = keep.tile([P, PACK, width], F32, name="h_%d_%d" % (c0, g))
             for t0 in range(0, PACK, BANK // width):
                 a, square = square_a(c0, width, g, t0)
                 at(step + 1, saturate, step + 1, c0, width, g, t0, a, square, h)
                 tick(step)
                 step = step + 1
-            at(step + 1, round_h, step + 1, n, c0, width, g, h)
-        for tail in range(step, step + 10):
+            at(step + 1, after_block, step + 2, c0, width, g, h)
+        for tail in range(step, step + TAIL_STEPS):
             tick(tail)

from contextlib import ExitStack

import concourse.mybir as mybir

K, T, S, H, N = 512, 4096, 1024, 1024, 512
FLOPS = 2 * (2 * K * H * S + 2 * H * N * S)

F32 = mybir.dt.float32
BF16 = mybir.dt.bfloat16
I32 = mybir.dt.int32
U32 = mybir.dt.uint32
U16 = mybir.dt.uint16
U8 = mybir.dt.uint8
FP8X4 = mybir.dt.float8_e4m3fn_x4
FP4X4 = mybir.dt.float4_e2m1fn_x4
ACT = mybir.ActivationFunctionType
ALU = mybir.AluOpType

P = 128
PACK = 4
PASS = P * PACK
BANK = 512
GROUPS = H // PASS
QUADRANTS = 4
HALF = S // 2
LIST_COLS = HALF // 16

BLOCKS = [(0, 512, 0), (0, 256, 1), (256, 256, 1), (512, 256, 0), (512, 256, 1),
          (768, 128, 0), (768, 128, 1), (896, 128, 0), (896, 128, 1)]
LAST = S - BLOCKS[-1][1]
SCALAR_PIECE = 128
EARLY = 768
TAIL_STEPS = 10


def tile_list_book_impact_kernel(tc, tab_words, tab_scales, offs, w1, w2_words, w2_scales, gain,
                                          w3, w4_words, w4_scales, base, out_0, out_1, out_2, out_3):
    nc = tc.nc
    with ExitStack() as ctx:
        keep = ctx.enter_context(tc.tile_pool(name="keep", bufs=1))
        ring = ctx.enter_context(tc.tile_pool(name="ring", bufs=3))
        psum = ctx.enter_context(tc.psum_pool(name="psum", bufs=1))

        offsets = keep.tile([P, S // 16], U16, name="offsets")
        nc.sync.dma_start(offsets[:], offs)

        w2_w = []
        for g in range(GROUPS):
            words = keep.tile([P, 2 * PASS], U8, name="w2_w%d" % g, tag=("slot_a", "slot_b")[g], align_bytes=64)
            nc.sync.dma_start(out=words[:].bitcast(I32),
                              in_=w2_words[0, :, 2 * PASS * g : 2 * PASS * (g + 1)].bitcast(I32))
            w2_w.append(words)

        def load_scale_rows(plane, rows):
            nc.vector.memset(plane[:].bitcast(I32), 0)
            for q in range(QUADRANTS):
                nc.scalar.dma_start(out=plane[32 * q : 32 * q + 4, :].bitcast(I32),
                                    in_=rows[4 * q : 4 * q + 4, :].bitcast(I32))

        tab_s = keep.tile([P, T], U8, name="tab_s", tag="slot_s", align_bytes=64)
        load_scale_rows(tab_s, tab_scales[0])

        one = keep.tile([P, 1], F32, name="one")
        nc.vector.memset(one[:], 1.0)
        warm = keep.tile([P, 1], F32, name="warm")
        nc.scalar.activation(warm[:], one[:], ACT.Abs_reciprocal_sqrt)

        w2_s = keep.tile([P, H], U8, name="w2_s", tag="slot_w", align_bytes=64)
        load_scale_rows(w2_s, w2_scales[0])

        gain_sb = keep.tile([P, GROUPS, PACK], F32, name="gain_sb")
        loaded = {}

        def load_table():
            loaded["tab"] = keep.tile([P, T], I32, name="tab_w", tag="slot_a", align_bytes=64)
            nc.sync.dma_start(out=loaded["tab"][:], in_=tab_words[0].rearrange("p n t -> p (n t)").bitcast(I32))

        def load_w1(g):
            loaded["w1", g] = keep.tile([P, PACK, PASS], F32, name="w1_raw%d" % g, tag=("slot_c", "slot_b")[g],
                                        align_bytes=64)
            nc.sync.dma_start(out=loaded["w1", g][:],
                              in_=w1.rearrange("(p j) c -> p j c", j=PACK)[:, :, PASS * g : PASS * (g + 1)])

        def load_w3(g):
            loaded["w3", g] = keep.tile([P, PACK, N], F32, name="w3_raw%d" % g, tag=("slot_s", "slot_a")[g],
                                        align_bytes=64)
            nc.sync.dma_start(out=loaded["w3", g][:],
                              in_=w3[PASS * g : PASS * (g + 1), :].rearrange("(p j) n -> p j n", j=PACK))

        def load_w4_words():
            loaded["w4_w"] = keep.tile([P, GROUPS, N], I32, name="w4_w", tag="slot_c", align_bytes=64)
            nc.sync.dma_start(out=loaded["w4_w"][:], in_=w4_words.rearrange("g p n t -> p g (n t)").bitcast(I32))

        def load_w4_scales():
            loaded["w4_s"] = keep.tile([P, GROUPS, N], U8, name="w4_s", tag="slot_w", align_bytes=64)
            for q in range(QUADRANTS):
                nc.sync.dma_start(out=loaded["w4_s"][32 * q : 32 * q + 4, :, :].bitcast(I32),
                                  in_=w4_scales[:, 4 * q : 4 * q + 4, :].rearrange("g r n -> r g n").bitcast(I32))

        def load_base():
            loaded["base"] = keep.tile([P, N // P, S], F32, name="base_sb", tag="slot_b", align_bytes=64)
            base_rows = base.rearrange("(i p) s -> p i s", p=P)
            for i0 in (0, 2):
                nc.sync.dma_start(out=loaded["base"][:, i0 : i0 + 2, :], in_=base_rows[:, i0 : i0 + 2, :])

        v_s = [keep.tile([P, HALF], U8, name="v_s%d" % half, align_bytes=64) for half in range(2)]
        v_w = [keep.tile([P, HALF], U32, name="v_w%d" % half, align_bytes=64) for half in range(2)]

        def gather_scales(half):
            entries = offsets[:, LIST_COLS * half : LIST_COLS * (half + 1)]
            nc.vector.tensor_copy(v_s[half][:], tab_s[:].indirect(entries))

        def gather_words(half):
            entries = offsets[:, LIST_COLS * half : LIST_COLS * (half + 1)]
            nc.vector.tensor_copy(v_w[half][:], loaded["tab"][:].bitcast(U32).indirect(entries))

        def looked_up(c0, width):
            half, v0 = divmod(c0, HALF)
            return v_w[half][:, v0 : v0 + width].bitcast(FP8X4), v_s[half][:, v0 : v0 + width]

        w2_wd = [keep.tile([P, 2 * PASS], U8, name="w2_wd%d" % g, align_bytes=64) for g in range(GROUPS)]
        w2_sd = [keep.tile([P, PASS], U8, name="w2_sd%d" % g, align_bytes=64) for g in range(GROUPS)]

        def deal_w2_words(g):
            nc.vector.tensor_copy(w2_wd[g][:].bitcast(U16).rearrange("p (t m) -> p t m", t=PACK),
                                  w2_w[g][:].bitcast(U16).rearrange("p (m t) -> p t m", t=PACK))

        def deal_w2_scales(g):
            nc.vector.tensor_copy(w2_sd[g][:].rearrange("p (t m) -> p t m", t=PACK),
                                  w2_s[:, PASS * g : PASS * (g + 1)].rearrange("p (m t) -> p t m", t=PACK))

        w1_q = [keep.tile([P, PASS], U32, name="w1_q%d" % g, align_bytes=64) for g in range(GROUPS)]
        w1_s = [keep.tile([P, PASS], U8, name="w1_s%d" % g, align_bytes=64) for g in range(GROUPS)]
        w1_b = [keep.tile([P, PACK * PASS], BF16, name="w1_b%d" % g, align_bytes=64) for g in range(GROUPS)]

        def round_w1(copy, g, m0, m1):
            copy(w1_b[g][:].rearrange("p (t m j) -> p m t j", t=PACK, j=PACK)[:, m0:m1],
                 loaded["w1", g][:].rearrange("p j (m t) -> p m t j", t=PACK)[:, m0:m1])

        def quantise_w1(g):
            nc.vector.quantize_mx(out=w1_q[g][:].bitcast(FP8X4), scales=w1_s[g][:], in_=w1_b[g][:])

        def weave(copy, dst, src, c0, c1):
            copy(dst[:, c0:c1, :].rearrange("p (c i) t -> p c t i", i=2),
                 src[:, :, c0:c1].rearrange("p t (c i) -> p c t i", i=2))

        w3_q = [keep.tile([P, N], U32, name="w3_q%d" % g, align_bytes=64) for g in range(GROUPS)]
        w3_s = [keep.tile([P, N], U8, name="w3_s%d" % g, align_bytes=64) for g in range(GROUPS)]
        w3_b = [keep.tile([P, N, PACK], BF16, name="w3_b%d" % g, align_bytes=64) for g in range(GROUPS)]

        def round_w3(g):
            weave(nc.vector.tensor_copy, w3_b[g], loaded["w3", g], 0, N)

        def quantise_w3(g):
            nc.vector.quantize_mx(out=w3_q[g][:].bitcast(FP8X4), scales=w3_s[g][:],
                                  in_=w3_b[g][:].rearrange("p n j -> p (n j)"))

        later = {}

        def at(step, work, *args):
            later.setdefault(step, []).append((work, args))

        def tick(step):
            for work, args in later.pop(step, []):
                work(*args)

        h_q = keep.tile([P, GROUPS * S], U32, name="h_q", align_bytes=64)
        h_s_early = keep.tile([P, GROUPS, EARLY], U8, name="h_s_early", align_bytes=64)
        h_s_late = keep.tile([P, GROUPS, S - EARLY], U8, name="h_s_late", align_bytes=64)

        def h_words(c0, width, g):
            return h_q[:, S * g + c0 : S * g + c0 + width]

        def h_scales(c0, width, g):
            if c0 < EARLY:
                return h_s_early[:, g, c0 : c0 + width]
            return h_s_late[:, g, c0 - EARLY : c0 - EARLY + width]

        def square_a(c0, width, g, t0):
            v_words, v_scales = looked_up(c0, width)
            per_bank = BANK // width
            a = psum.tile([P, per_bank, width], F32, name="a", tag="a", bufs=4)
            for i in range(per_bank):
                t = t0 + i
                nc.tensor.matmul_mx(out=a[:, i, :], lhsT=w1_q[g][:, P * t : P * (t + 1)].bitcast(FP8X4),
                                    lhsT_scale=w1_s[g][:, P * t : P * (t + 1)],
                                    rhs=v_words, rhs_scale=v_scales, start=True, stop=True)
            square = ring.tile([P, per_bank, width], F32, name="square")
            nc.scalar.activation(square[:], a[:], ACT.Square)
            return a, square

        def saturate(step, c0, width, g, t0, a, square, h):
            per_bank = BANK // width
            root = ring.tile([P, per_bank, width], F32, name="root")
            nc.scalar.activation(root[:], square[:], ACT.Abs_reciprocal_sqrt, bias=one[:])
            sat = ring.tile([P, per_bank, width], F32, name="sat")
            for i in range(per_bank):
                t = t0 + i
                nc.vector.scalar_tensor_tensor(sat[:, i, :], a[:, i, :], gain_sb[:, g, t : t + 1], root[:, i, :],
                                               ALU.mult, ALU.mult)
            at(step + 1, add_linear, c0, width, g, t0, sat, h)

        def add_linear(c0, width, g, t0, sat, h):
            v_words, v_scales = looked_up(c0, width)
            per_bank = BANK // width
            b = psum.tile([P, per_bank, width], F32, name="b", bufs=2)
            for i in range(per_bank):
                t = t0 + i
                nc.tensor.matmul_mx(out=b[:, i, :], lhsT=w2_wd[g][:, 2 * P * t : 2 * P * (t + 1)].bitcast(FP4X4),
                                    lhsT_scale=w2_sd[g][:, P * t : P * (t + 1)],
                                    rhs=v_words, rhs_scale=v_scales, start=True, stop=True)
            nc.vector.tensor_tensor(h[:, t0 : t0 + per_bank, :], sat[:], b[:], ALU.add)
            if t0 + per_bank == PACK:
                nc.sync.dma_start(
                    out=out_1[PASS * g : PASS * (g + 1), c0 : c0 + width].rearrange("(p t) s -> p t s", t=PACK),
                    in_=h[:])

        def store_scales(plane, c0, c1):
            for q in range(QUADRANTS):
                nc.sync.dma_start(out=out_3[:, 4 * q : 4 * q + 4, c0:c1].rearrange("g r m -> r g m").bitcast(I32),
                                  in_=plane[32 * q : 32 * q + 4, :, :].bitcast(I32))

        def quantise_h(c0, width, g, h_b):
            nc.vector.quantize_mx(out=h_words(c0, width, g).bitcast(FP8X4), scales=h_scales(c0, width, g),
                                  in_=h_b[:].rearrange("p s t -> p (s t)"))
            nc.sync.dma_start(out=out_2[g, :, c0 : c0 + width, :].rearrange("p m t -> p (m t)").bitcast(I32),
                              in_=h_words(c0, width, g).bitcast(I32))
            if g == GROUPS - 1 and c0 + width == EARLY:
                store_scales(h_s_early, 0, EARLY)
            if g == GROUPS - 1 and c0 + width == S:
                store_scales(h_s_late, EARLY, S)

        def after_block(step, c0, width, g, h):
            h_b = ring.tile([P, width, PACK], BF16, name="h_b", align_bytes=64)
            if c0 < LAST:
                pieces = width // SCALAR_PIECE
                for i in range(pieces):
                    at(step + i // 2, weave, nc.scalar.copy, h_b, h, SCALAR_PIECE * i, SCALAR_PIECE * (i + 1))
                rounded = step + (pieces - 1) // 2
            else:
                at(step, weave, nc.vector.tensor_copy, h_b, h, 0, width)
                rounded = step
            at(rounded + 1, quantise_h, c0, width, g, h_b)
            if c0 == LAST:
                at(rounded + 2, last_readings, g, c0, width)
            elif g == GROUPS - 1:
                y = keep.tile([P, N // P, width], F32, name="y_%d" % c0)
                for m, i0 in enumerate(range(0, N // P, BANK // width)):
                    at(rounded + 2 + m, readings, rounded + 2 + m, c0, width, i0, y)

        def reading_weights():
            return (([w3_q[g][:] for g in range(GROUPS)], [w3_s[g][:] for g in range(GROUPS)]),
                    ([loaded["w4_w"][:, g, :] for g in range(GROUPS)], [loaded["w4_s"][:, g, :] for g in range(GROUPS)]))

        def reading_pass(out, words, scales, i, c0, width, g, start, stop):
            cols = slice(P * i, P * (i + 1))
            nc.tensor.matmul_mx(out=out, lhsT=words[g][:, cols].bitcast(FP8X4), lhsT_scale=scales[g][:, cols],
                                rhs=h_words(c0, width, g).bitcast(FP8X4), rhs_scale=h_scales(c0, width, g),
                                start=start, stop=stop)

        def multiply(d, e, count, width):
            d_sb = ring.tile([P, count, width], F32, name="d_sb")
            nc.scalar.copy(d_sb[:], d[:])
            prod = ring.tile([P, count, width], F32, name="prod")
            nc.vector.tensor_tensor(prod[:], d_sb[:], e[:], ALU.mult)
            return prod

        def less_base(c0, width, i0, count, prod, y):
            rows = slice(i0, i0 + count)
            if c0 < EARLY:
                for i in range(count):
                    nc.gpsimd.tensor_tensor(y[:, i0 + i, :], prod[:, i, :], loaded["base"][:, i0 + i, c0 : c0 + width],
                                            ALU.subtract)
            else:
                nc.vector.tensor_tensor(y[:, rows, :], prod[:], loaded["base"][:, rows, c0 : c0 + width], ALU.subtract)
            nc.sync.dma_start(out=out_0.rearrange("(i p) s -> p i s", p=P)[:, rows, c0 : c0 + width], in_=y[:, rows, :])

        def readings(step, c0, width, i0, y):
            per_bank = BANK // width
            d = psum.tile([P, per_bank, width], F32, name="d", bufs=1)
            e = psum.tile([P, per_bank, width], F32, name="e", bufs=1)
            for bank, (words, scales) in zip((d, e), reading_weights()):
                for i in range(per_bank):
                    for g in range(GROUPS):
                        reading_pass(bank[:, i, :], words, scales, i0 + i, c0, width, g, g == 0, g == GROUPS - 1)
            at(step + 1, less_base, c0, width, i0, per_bank, multiply(d, e, per_bank, width), y)

        last_banks = {}

        def last_readings(g, c0, width):
            for i0 in (0, 2):
                for r, (words, scales) in enumerate(reading_weights()):
                    if g == 0:
                        last_banks[i0, r] = psum.tile([P, 2, width], F32, name="last_%d_%d" % (i0, r), tag="a", bufs=4)
                    for i in range(2):
                        reading_pass(last_banks[i0, r][:, i, :], words, scales, i0 + i, c0, width, g,
                                     g == 0 and i == 0, g == GROUPS - 1 and i == 1)
            if g == GROUPS - 1:
                y = keep.tile([P, N // P, width], F32, name="y_%d" % c0)
                prods = [multiply(last_banks[i0, 0], last_banks[i0, 1], 2, width) for i0 in (0, 2)]
                for i0, prod in zip((0, 2), prods):
                    less_base(c0, width, i0, 2, prod, y)

        load_w1(0)
        nc.sync.dma_start(out=gain_sb[:], in_=gain.rearrange("(g p t) -> p g t", g=GROUPS, t=PACK))
        deal_w2_words(0)
        load_table()
        deal_w2_words(1)
        load_w1(1)
        gather_scales(0)
        round_w1(nc.vector.tensor_copy, 0, 0, P)
        gather_scales(1)
        quantise_w1(0)
        load_w3(0)
        load_w4_words()
        deal_w2_scales(0)
        deal_w2_scales(1)
        load_w4_scales()
        gather_words(0)

        at(0, gather_words, 1)
        at(0, load_w3, 1)
        for i in range(4):
            at(1 + i // 2, round_w1, nc.scalar.copy, 1, 32 * i, 32 * (i + 1))
        at(3, quantise_w1, 1)
        at(3, load_base)
        for g in range(GROUPS):
            at(3 + 2 * g, round_w3, g)
            at(4 + 2 * g, quantise_w3, g)

        step = 0
        for c0, width, g in BLOCKS:
            h = keep.tile([P, PACK, width], F32, name="h_%d_%d" % (c0, g))
            for t0 in range(0, PACK, BANK // width):
                a, square = square_a(c0, width, g, t0)
                at(step + 1, saturate, step + 1, c0, width, g, t0, a, square, h)
                tick(step)
                step = step + 1
            at(step + 1, after_block, step + 2, c0, width, g, h)
        for tail in range(step, step + TAIL_STEPS):
            tick(tail)
